import numpy as np, ml_dtypes
CORES = [2,3,42,43,82,83,122,123]
N = 8
BF = ml_dtypes.bfloat16
def gentries(a):
    return np.ascontiguousarray(a.reshape(8, 16, -1).transpose(0, 2, 1)).reshape(8, -1)
def gtable(e):
    e = np.asarray(e); return np.ascontiguousarray(e.reshape(8, -1, 16).transpose(0, 2, 1)).reshape(128, -1).astype(np.int32)
E, V, XB, K0, RO = 2048, 1024, 7, 4, 2
MASKS = [1, 2]
C, TOP, OFF = 2 ** K0, 2 ** XB - 1, 64 * 2 ** XB
def cut(rng, n, m):
    return np.repeat(np.arange(len(n)), n)[:m][rng.permutation(m)]
def ring(rng, cid):
    o = np.lexsort((rng.random(E), cid)); c = cid[o]
    st = np.flatnonzero(np.concatenate([np.array([True]), c[1:] != c[:-1]])); n = np.diff(np.append(st, E))
    nx = np.arange(1, E + 1); nx[np.append(st[1:], E) - 1] = st
    s, l, p = np.empty(E, np.int64), np.empty(E, np.int64), np.empty(E, np.int64)
    s[o] = o[nx]; l[o] = np.repeat(np.minimum.reduceat(o, st), n); p[o] = np.arange(E) - np.repeat(st, n)
    return s, l, p
def rings(rng, cid):
    s, l, p = np.empty(cid.shape, np.int64), np.empty(cid.shape, np.int64), np.empty(cid.shape, np.int64)
    for q in range(N):
        for g in range(8): s[q, g], l[q, g], p[q, g] = ring(rng, cid[q, g])
    return s, l, p
def deal(rng):
    return np.stack([np.stack([cut(rng, np.append(C, rng.integers(1, C + 1, E)), E) for g in range(8)]) for q in range(N)])
def levels(rng, l):
    w = rng.random((N, 8, 16, 1)); lev = np.take_along_axis(rng.random((N, 8, 16, E)), l[:, :, None, :], 3)
    return np.minimum((2 ** XB * (w * lev + (1 - w) * rng.random((N, 8, 16, E)))).astype(np.int64), TOP)
def chains(rng):
    n = 5 * V // 16; o = np.sort(np.append(0, 1 + rng.permutation(V - 1))[:3 * n].reshape(n, 3), axis=1); d = 2 * o + rng.integers(0, 2, (n, 3)); c = np.arange(E)
    c[d[:, 0]] = d[:, 1]; c[d[:, 0] ^ 1] = d[:, 2]
    return c
def graded(rng):
    o = rng.permutation(V); n = V // 8; c = np.arange(E); x = np.zeros((16, E), np.int64)
    a, b, d = o[:n], o[n:2 * n], o[2 * n:3 * n]; c[2 * a] = 2 * d; c[2 * a + 1] = 2 * b; c[2 * b + 1] = 2 * d + 1
    y = rng.integers(2 ** (XB - 1) + 1, TOP, (16, n)); up = rng.integers(0, 2, (16, n)); up[0] = 1
    x[:, 2 * d] = y + up; x[:, 2 * b + 1] = y; x[:, 2 * a + 1] = TOP
    a, b = o[3 * n::2], o[3 * n + 1::2]; c[2 * a + 1] = 2 * b
    y = rng.integers(2 ** (XB - 1) + 1, TOP, (16, len(a))); up = rng.integers(0, 2, y.shape); up[0] = 1
    x[:, 2 * a] = y; x[:, 2 * b + 1] = y + up
    return c, x
def pack(x, s, l):
    return {"x0": np.ascontiguousarray(x.reshape(N, 128, E)).astype(np.float32).astype(BF), "su": np.stack([gtable(a) for a in s]), "lab": l.astype(np.int32)}
def setup_inputs(rng):
    s, l, p = rings(rng, deal(rng))
    return pack(levels(rng, l), s, l)
def setup_inputs_full(rng):
    cid = np.empty((N, 8, E), np.int64); n = E // C
    for q in range(N):
        for g in range(8):
            if g & 1: cid[q, g] = cut(rng, np.full(n, C), E); continue
            c = np.full(E, -1, np.int64); top = V - 1
            for t in range(RO):
                w = 2 ** (t + 1); k = np.arange(n // w); flip = rng.integers(0, 2, len(k)); e = 2 * (top - k)
                c[e + flip] = w * k + rng.integers(0, w // 2, len(k)); c[e + 1 - flip] = w * k + w // 2 + rng.integers(0, w // 2, len(k)); top -= n // w
            free = np.repeat(np.arange(n), C - np.bincount(c[c >= 0], minlength=n))
            c[c < 0] = rng.permutation(free); cid[q, g] = c
    s, l, p = rings(rng, cid); x = levels(rng, l); x[:, ::2] = rng.integers(1, TOP + 1, (1, 4, 1, 1))
    return pack(x, s, l)
def setup_inputs_ties(rng):
    cid = deal(rng)
    cid[0, 0] = cut(rng, np.full(E // C, C), E)
    cid[0, 1, 0::2] = 2 * cut(rng, rng.integers(1, C + 1, V), V); cid[0, 1, 1::2] = 2 * cut(rng, rng.integers(1, C + 1, V), V) + 1
    cid[0, 1, 0] = E; cid[0, 1, 1] = E + 1
    for q in range(N): cid[q, 4] = chains(rng)
    cid[0, 6], lev = graded(rng)
    s, l, p = rings(rng, cid)
    for a in (s, l, p): a[:, [0, 1, 6]] = a[0:1, [0, 1, 6]].copy()
    x = TOP * rng.integers(0, 2, (N, 8, 16, E))
    x[:, 0] = TOP * (p[:, 0, None, :] & 1); x[:, 1] = TOP * (1 - (np.arange(E) & 1))
    x[:, 2:4] = rng.integers(0, 2, (N, 2, 16, E)); x[:, 4:6] = rng.integers(0, TOP + 1, (N, 2, 1, 1)); x[:, 6] = lev
    return pack(x, s, l)
def setup_inputs_ends(rng):
    cid = deal(rng); e = np.arange(E)
    shut = rng.permutation(np.concatenate([np.array([0, 7]), 1 + rng.permutation(6)])[:N]); z = int(rng.choice(np.flatnonzero(shut < 7)))
    for q in range(N):
        k = rng.permutation(8); i = int(np.flatnonzero(k == 3)[0]); k[i] = k[shut[q]]; k[shut[q]] = 3
        if q == z: k = np.where(k == 3, 3, 0); k[7] = 7
        for g in range(8):
            if k[g] == 0: cid[q, g] = e
            if k[g] in (1, 2, 3, 6): cid[q, g] = np.repeat(cut(rng, rng.integers(1, C // 2 + 1, V), V), 2)
            if k[g] == 1: cid[q, g, 0] = E; cid[q, g, 1] = E + 1
            if k[g] == 2: cid[q, g, E - 2] = E; cid[q, g, E - 1] = E + 1
            if k[g] == 4: cid[q, g] = cut(rng, np.full(E // C, C), E)
            if k[g] == 5: cid[q, g] = ((e + 1) >> 1) & (V - 1)
            if k[g] == 6: cid[q, g, V:] = E + cut(rng, rng.integers(1, C + 1, V), V)
    s, l, p = rings(rng, cid)
    return pack(levels(rng, l), s, l)
def setup_inputs_spread(rng):
    cid = np.stack([np.stack([cut(rng, np.minimum(np.exp2((K0 + 1) * rng.random(E)).astype(np.int64), C), E) for g in range(8)]) for q in range(N)])
    s, l, p = rings(rng, cid)
    x = np.exp2((XB + 1) * rng.random((N, 8, 1, E))) * rng.random((N, 8, 16, E)) * (rng.random((N, 8, 1, E)) > 0.0625)
    return pack(np.minimum(x.astype(np.int64), TOP), s, l)
def check_inputs(d):
    bad = []; x = np.asarray(d["x0"]).astype(np.float32)
    if not np.all((x >= 0) & (x <= TOP) & (x == np.floor(x))): bad.append("range of x0")
    if np.min(d["su"]) < 0 or np.max(d["su"]) >= E: return bad + ["range of su"]
    s = np.stack([gentries(a) for a in d["su"]]).astype(np.int64); e = np.broadcast_to(np.arange(E), s.shape)
    if not np.array_equal(np.sort(s, axis=2), e): bad.append("su is no permutation")
    cur, low, back = e, e, np.zeros(s.shape, bool)
    for t in range(C):
        cur = np.take_along_axis(s, cur, 2); low = np.minimum(low, cur); back = back | (cur == e)
    if not np.all(back): bad.append("a circuit of su is too long")
    if not np.array_equal(low, np.asarray(d["lab"])): bad.append("lab is not the lowest edge of the circuit")
    return bad
def reference(x0, su, lab):
    x = x0.astype(np.float32).astype(np.int64).reshape(N, 8, 16, E)
    s = np.stack([gentries(a) for a in su]).astype(np.int64); l = lab.astype(np.int64); v = np.arange(V)
    for t in range(RO):
        K = K0 + t; gain = np.zeros((N, 8, V), np.int64)
        for y in (x, x[np.arange(N) ^ MASKS[t]]):
            o = np.take_along_axis(y, s[:, :, None, :], 3)
            i0, i1, o0, o1 = y[..., 0::2], y[..., 1::2], o[..., 0::2], o[..., 1::2]
            gain = gain + np.add.reduce(np.abs(i0 - o0) + np.abs(i1 - o1) - np.abs(i0 - o1) - np.abs(i1 - o0), axis=2)
        l0, l1 = l[..., 0::2], l[..., 1::2]
        key = np.where(l0 != l1, V * (gain + OFF) + v, 0)
        b, a, j = np.repeat(key, 2, axis=2), x, s
        for k in range(K):
            a = a + np.take_along_axis(a, j[:, :, None, :], 3)
            b = np.maximum(b, np.take_along_axis(b, j, 2))
            j = np.take_along_axis(j, j, 2)
        merge = (key > 0) & (b[..., 0::2] == key) & (b[..., 1::2] == key)
        s0, s1 = s[..., 0::2], s[..., 1::2]
        s = np.stack([np.where(merge, s1, s0), np.where(merge, s0, s1)], axis=3).reshape(N, 8, E)
        low = np.where(merge, np.minimum(l0, l1), E)
        l = np.where(b > 0, np.minimum(l, np.take_along_axis(low, b & (V - 1), 2)), l)
        x = a >> K
    return {"ysu": s.astype(np.float32), "ylab": l.astype(np.float32), "yx": x.reshape(N, 128, E).astype(np.float32).astype(BF)}

@@ -1,0 +1,530 @@
+from concourse.bass import DstId, RemoteDMATransfer
+from concourse.mybir import dt, AluOpType, AxisListType, ActivationFunctionType
+
+F, B, H, I, U = "float32", "bfloat16", "float16", "int32", "uint16"
+SCRATCH = {}
+for _d, _w, _names in [
+    (B, 2048, "x0s x0c x1n x1c og oh yb yo a1 a1c j0 ja jb tg"), (B, 4096, "rr mm"), (B, 1040, "tw"), (B, 2064, "xm"), (H, 2048, "lrow"),
+    (F, 2048, "aa ab ac ba bc"), (F, 2064, "bb"), (F, 1024, "key kc"), (F, 272, "pm"),
+    (B, 128, "onesb zb idb idn idm ids hib lob"), (B, 144, "wd wdn"), (F, 144, "id32 wf s8f"), (H, 144, "idh s8h"),
+    (F, 8, "gm1 gm gm0"), (I, 4, "pcol pand"), (F, 4, "pmf"), (F, 16, "i16 sel16"),
+    (F, 128, "ones suf t1 t2 t3 sn qf qf2 labf lc l1 lf sf os1 os2"), (I, 128, "su32 si vi bq lo lab32 bi wv"), (H, 128, "labh"),
+    (U, 128, "ln lq lv lw lq2 lw2 lt lm p1 p2 k1 k2 k3 n1 n2 n3 n4"),
+    (F, 64, "v16 vp1 dq ds md gout1 gout2 gin1 gin2 eq ee iq m1 m2 ts"), (H, 64, "vph gh"), (I, 64, "ti thi tlo"), (B, 64, "thb tlb"),
+]:
+    for _n in _names.split():
+        SCRATCH[_n] = ("sbuf", [128, _w], _d)
+SCRATCH["cm"] = ("sbuf", [128, 2, 8, 64], F)
+SCRATCH["cn"] = ("sbuf", [128, 2, 8, 64], F)
+PS = ["d0", "d1", "d2", "kp0", "kp1", "gs", "e0", "e1"]
+for _n in PS:
+    SCRATCH[_n] = ("psum", [128, 512], F)
+SEMAPHORES = "cv ca cp cg sent ap1 ap2 ag1 ag2 qsu qx qxc qlab qrow qh ql qy2 qy3 qk0 qk1 qx0 qx1".split()
+SEMAPHORES += ["q%s%d" % (_n, _c) for _n in "abco" for _c in range(4)]
+A = AluOpType
+AF = ActivationFunctionType
+PAR = dict(cy=1.0e-3, gather=1.56, pe=0.5e-3, fix=0.06, dma=2.0, bw=2.0e5, rem=3.0, first=2.0, hop=0.1, look=0.1,
+           ca=[1, 0, 0, 0, 0, 0, 0, 0], cb=[0] * 6, kc=[1, 1], nq=4, s1=1, s2=1, own1=2, par1=0, own2=1, par2=2, yo=0, cn=4)
+WEIGHT = {4:4,47:21,71:20,113:3,124:10,127:20,135:9,137:28,139:23,151:16,161:11,167:-14,175:-16,181:6,187:-15,191:-7,194:17,200:-15,202:25,203:27,205:8,206:-9,209:14,261:-7,268:-5,269:28,270:10,279:-15,280:-34,286:-24,288:16,290:-3,301:-7,303:-8,305:-3,308:5,309:8,311:4,312:-2,315:9,316:-12,320:-9,322:-7,333:-8,346:-20,347:8,351:7,352:-19,354:3,357:5,378:-22,386:14,395:23,397:-10,399:-3,405:-9,407:10,408:-6,410:13,415:-5,421:-9,422:-1,424:-13,431:8,432:14,440:1,443:5,448:2,450:-8,457:-5,463:4,467:-1,470:-7,477:-11,480:13,487:6,492:-4,494:4,496:-10,498:-5,499:-20,500:6,501:6,503:13,504:-5,505:36,508:-7,511:8,555:1,556:1,574:16,595:2,646:1,663:8,665:4,666:22,701:-18,703:2,704:5,708:4,709:-3,714:2,715:6,718:-7,732:18,735:-16,736:3,737:-9,738:4,744:-3,745:13,748:-8,753:-10,755:-7,757:-15,759:1,766:-11,770:-6,773:-4,776:12,777:-12,778:16,779:-4,780:-5,781:13,793:2,794:2,795:20,797:6,798:2,800:2,802:7,803:4,804:-16,807:1,809:4,811:13,814:4,815:-3,816:7,817:-3,819:12,820:10,822:13,824:10,825:-4,826:1,827:-2,828:-5,830:8,833:-8,836:18,837:-2,839:-2,840:14,841:-2,842:-5,843:-5,844:2,845:-3,846:21,847:3,848:11,849:3,851:-12,856:-20,857:-6,862:-34,882:-16,887:-29,899:-7,933:-25,934:27,978:5,986:-14,988:29,991:15,998:14,1007:26,1083:-10,1084:5,1159:-24,1160:-30,1164:-6,1167:-7,1170:12,1182:3,1215:3,1216:2,1217:-2,1222:1,1223:3,1224:5,1225:9,1233:-4,1234:2,1235:1,1238:1,1239:12,1246:2,1251:-9,1254:3,1255:4,1257:-14,1260:-12,1263:-8,1264:-10,1265:8,1268:-10,1269:-1,1270:-20,1274:-2,1279:-18,1280:3,1283:-9,1285:-7,1287:-19}
+ORDER = {}
+
+
+def place(ops, pred, succ, prio, back=False):
+    n = len(ops)
+    left = [len(p) for p in pred]
+    est = [0.0] * n
+    ready = {q: [] for q in "vapgsx"}
+    free = {q: 0.0 for q in "vapgsx"}
+    for k in range(n):
+        if not left[k]:
+            ready[ops[k][0]].append(k)
+    order = []
+    while len(order) < n:
+        best = None
+        for q in ready:
+            if ready[q]:
+                t0 = max(free[q], min(est[k] for k in ready[q]))
+                if best is None or t0 < best[0]:
+                    best = (t0, q)
+        t0, q = best
+        k = max((k for k in ready[q] if est[k] <= t0 + PAR["look"]), key=lambda k: (prio[k], -k))
+        ready[q].remove(k)
+        st = max(free[q], est[k])
+        free[q] = st + ops[k][7]
+        order.append(k)
+        for s in succ[k]:
+            est[s] = max(est[s], st + ops[k][6] + (0.0 if ops[s][0] == q == "p" else PAR["hop"]))
+            left[s] -= 1
+            if not left[s]:
+                ready[ops[s][0]].append(s)
+    return (order,)
+
+
+def schedule(ops, deps):
+    n = len(ops)
+    succ = [[] for _ in range(n)]
+    for k in range(n):
+        for m in deps[k]:
+            succ[m].append(k)
+    pr = [0.0] * n
+    for k in range(n - 1, -1, -1):
+        pr[k] = ops[k][6] + WEIGHT.get(k, 0) + max([pr[s] + 0.1 for s in succ[k]] + [0.0])
+    return place(ops, deps, succ, pr)[0]
+
+
+def rank_program(g, core, T, topo):
+    rank = T.rank_of(core)
+    if rank is None:
+        return
+    eng = {"v": g.vector, "a": g.scalar, "p": g.tensor, "g": g, "s": g.sync}
+    csem = {"v": "cv", "a": "ca", "p": "cp", "g": "cg"}
+    ops = []
+    cy, fix = PAR["cy"], PAR["fix"]
+    size = {F: 4, B: 2, H: 2, I: 4, U: 2}
+
+    def v(name, a=None, b=None, s=None, p=None):
+        w = SCRATCH[name][1][1]
+        a = 0 if a is None else a
+        b = w if b is None else b
+        ps = slice(None) if p is None else slice(p[0], p[1], p[2] if len(p) > 2 else None)
+        return (T[name][ps, a:b:s] if s else T[name][ps, a:b], [(name, a, b, p)], len(range(a, b, s or 1)), size[SCRATCH[name][2]], name in PS)
+
+    def blk(name, c, n=512, p=None): return v(name, n * c, n * c + n, p=p)
+
+    def ind(win, lst, c, d):
+        return (T[win][:, 0:SCRATCH[win][1][1]].indirect(T[lst][:, c:d]), [(win, 0, 1 << 20, None), (lst, c, d, None)], 16 * (d - c), 4, "ind")
+
+    def rec(q, fn, reads, writes, lat, sem=None, kind="c", busy=None, after=()):
+        ops.append([q, fn, sum([r[1] for r in reads], []), sum([w[1] for w in writes], []), sem, kind, lat, lat if busy is None else busy, list(after)])
+        return len(ops) - 1
+
+    def cost(o, i, mult=1.0, half=True):
+        if i[4] == "ind":
+            return fix + i[2] * PAR["gather"] * cy
+        if half and o[3] == 2 and i[3] == 2:
+            mult = mult / 2
+        return fix + max(64, i[2] * mult) * cy
+
+    def copy(o, i): rec("v", lambda e: e.tensor_copy(o[0], i[0]), [i], [o], cost(o, i))
+    def tt(o, a, b, op): rec("v", lambda e: e.tensor_tensor(o[0], a[0], b[0], op), [a, b], [o], cost(o, a, 1 if a[4] or b[4] else 2, False))
+    def mset(o, c): rec("v", lambda e: e.memset(o[0], c), [], [o], cost(o, o))
+
+    def ts(o, a, s1, op0, s2=None, op1=None):
+        rd = [a] + [s for s in (s1, s2) if isinstance(s, tuple)]
+        x1 = s1[0] if isinstance(s1, tuple) else s1
+        if op1 is None:
+            rec("v", lambda e: e.tensor_scalar(o[0], a[0], x1, None, op0), rd, [o], cost(o, a))
+        else:
+            rec("v", lambda e: e.tensor_scalar(o[0], a[0], x1, s2, op0, op1), rd, [o], cost(o, a))
+
+    def act(o, i, func=None, bias=0.0, scale=1.0):
+        f = AF.Identity if func is None else func
+        rd = [i] + ([scale] if isinstance(scale, tuple) else [])
+        sc = scale[0] if isinstance(scale, tuple) else scale
+        rec("a", lambda e: e.activation(o[0], i[0], f, bias=bias, scale=sc), rd, [o], cost(o, i, 1, False))
+
+    def mm(o, l, r, st, sp):
+        rec("p", lambda e: e.matmul(o[0], l[0], r[0], st, sp), [l, r], [o], max(min(64, l[2]), r[2]) * l[3] * l[3] / 4 * PAR["pe"])
+
+    def aff(o, i, pat, cmp, base, cm): rec("g", lambda e: e.affine_select(o[0], i[0], pat, cmp, 0.0, base, cm), [i], [o], 0.17 + 2 * o[2] * cy)
+
+    def iota(o, pat, base, cm, fl):
+        if fl:
+            rec("g", lambda e: e.iota(o[0], pat, base, cm, allow_small_or_imprecise_dtypes=True), [], [o], 0.13 + 2 * o[2] * cy)
+        else:
+            rec("g", lambda e: e.iota(o[0], pat, base, cm), [], [o], 0.13 + 2 * o[2] * cy)
+
+    def dma(q, o, i, sem, kb):
+        t = kb * 1024 / PAR["bw"]
+        rec(q, lambda e: e.dma_start(o[0], i[0]), [i], [o], PAR["dma"] + t, sem, "d", max(0.1, t) if q == "s" else 0.1)
+
+    def hbm(ap): return (ap, [])
+    ROW = (0, 128, 16)
+
+    pa = [T.cores[rank ^ 1], T.cores[rank ^ 2]]
+    use = [e for e in topo.engines(core, pa[0]) if e in topo.engines(core, pa[1])][:8]
+    emask = sum(1 << e for e in use)
+    nsent = [0]
+
+    def exchange(src, dst, r, sem):
+        rid, pid, _se = topo.addr(pa[r])
+        ex = 0.0 if nsent[0] else PAR["first"]
+        nsent[0] += len(use)
+        k = rec("g", lambda e: e.remote_dma(T[dst][:], T[src][:], T.sem[sem], T.sem.sent, pid, rid, emask), [v(src)], [], PAR["rem"] + ex, "sent", "r", 0.5 + ex)
+        rec("x", None, [], [v(dst)], 0.0, sem, "x", after=[k])
+
+    def extract(ps, src, h, mask="wd"):
+        for i in range(16):
+            mm(blk(ps, h, 64), v(mask, 15 - i, 143 - i), v(src, 1024 * h + i, 1024 * (h + 1), 16), i == 0, i == 15)
+
+    def jstep(out, win, lst, ps):
+        for h in range(2):
+            act(blk(out, h, 1024), ind(win, lst, 64 * h, 64 * h + 64))
+            extract(ps, out, h)
+
+    def second(out, c, step):
+        if c >= 4 - PAR["ca"][step]:
+            act(blk("ac", c), blk(out, c))
+        else:
+            dma("s", blk("ac", c), blk(out, c), "qa%d" % c, 256)
+
+    def astep(out, win, in1, lst, keep, step):
+        for c in range(4):
+            tt(blk(out, c), ind(win, lst, 32 * c, 32 * c + 32), blk(in1, c), A.add)
+            if keep:
+                second(out, c, step)
+
+    def bstep(out, win, lst, keep, first=False):
+        for c in range(4):
+            tt(blk(out, c), ind(win, lst, 32 * c, 32 * c + 32), blk("kc", c % 2) if first else blk("bc", c), A.max)
+            if keep and c >= 4 - PAR["cb"][nb[0]]:
+                act(blk("bc", c), blk(out, c))
+            elif keep:
+                dma("s", blk("bc", c, p=ROW), blk(out, c, p=ROW), "qb%d" % c, 16)
+        nb[0] += 1 if keep else 0
+
+    TERMS = [(0, 0, "wd"), (1, 0, "wdn"), (1, 1, "wd"), (0, 1, "wdn")]
+    dn, nb = [0], [0]
+
+    def bank():
+        dn[0] += 1
+        return "d%d" % (dn[0] % 3)
+
+    def own_x(r, b, a, n, sec=False):
+        if r == 0:
+            return v("x0c" if sec else "x0s", 2 * a + b, 2 * (a + n), 2)
+        return v("x1c" if sec else "x1n", 1024 * b + a, 1024 * b + a + n)
+
+    def gather_o(og, win, lst, h): act(blk(og, h, 1024), ind(win, lst, 64 * h, 64 * h + 64))
+
+    def gains(r, lst, own, nact, gathered=False):
+        rr, og, win = ("rr" if own else "mm"), ("og" if own else "oh"), ("x0s", "x1n")[r]
+        for k in range(4):
+            b, h, mask = TERMS[k]
+            if h < nact and k % 2 == 0 and not gathered:
+                gather_o(og, win, lst, h)
+            for hf in range(2):
+                o = blk(rr, 2 * k + hf)
+                if h < nact:
+                    d = bank()
+                    mm(v(d), v("idb"), own_x(r, b, 512 * hf, 512), True, False)
+                    mm(v(d), v("idn"), blk(og, 2 * h + hf), False, True)
+                    act(o, v(d), AF.Relu)
+                else:
+                    tt(o, ind(win, lst, 64 * h + 32 * hf, 64 * h + 32 * hf + 32), own_x(r, b, 512 * hf, 512, True), A.max)
+                if own:
+                    mm(v("kp%d" % hf), v(mask, 15, 143), o, False, False)
+            if not own:
+                for i in range(16):
+                    mm(v("gs", 0, 64), v(mask, 15 - i, 143 - i), v(rr, 1024 * k + i, 1024 * (k + 1), 16), k == 0 and i == 0, k == 3 and i == 15)
+
+    def first_sums(r, out, lst, gathered):
+        for c in range(4):
+            if c % 2 == 0 and not gathered:
+                gather_o("og", "x1n", lst, c // 2)
+            d = bank()
+            mm(v(d), v("idb"), own_x(r, c // 2, 512 * (c % 2), 512), True, False)
+            mm(v(d), v("idb"), blk("og", c), False, True)
+            act(blk(out, c), v(d))
+            if r:
+                second(out, c, 2)
+
+    def kclear(hf): mm(v("kp%d" % hf), v("zb"), v("x0s", 0, 512), True, False)
+
+    def expand16(src, hf, last):
+        for i in range(16):
+            mm(v("kp%d" % hf, i, 512, 16), v("idh", i, i + 128), blk(src, hf, 32), False, last and i == 15)
+
+    def keyout(r):
+        for hf in range(2):
+            expand16("gh", hf, True)
+            act(blk("key", hf), v("kp%d" % hf), AF.Relu, bias=4096.0)
+            if PAR["kc"][r]:
+                act(blk("kc", hf), v("kp%d" % hf), AF.Relu, bias=4096.0)
+            else:
+                dma("s", blk("kc", hf, p=ROW), blk("key", hf, p=ROW), "qk%d" % hf, 16)
+
+    def twindow():
+        for hf in range(2):
+            kclear(hf)
+            for r, src in ((0, "thb"), (1, "tlb")):
+                for i in range(16):
+                    mm(v("kp%d" % hf, i, 512, 16), v("xm", 16 - r + 128 * i, 144 - r + 128 * i), blk(src, hf, 32), False, r == 1 and i == 15)
+            act(v("tw", 1 + 512 * hf, 513 + 512 * hf), v("kp%d" % hf))
+
+    def jwindow(q, lw, ps):
+        ts(v("lob"), v("lo"), 1.0, A.mult)
+        dma("s", v("j0", p=(1, 128, 16)), v("lob"), "ql", 32)
+        tt(v("hib"), v(q), v("lo"), A.subtract)
+        dma("s", v("j0", p=ROW), v("hib"), "qh", 32)
+        mm(v(ps, 0, 128), v("idm"), v("lob"), True, False)
+        mm(v(ps, 0, 128), v("ids"), v("hib"), False, True)
+        copy(v(lw), v(ps, 0, 128))
+
+    def ev(n): return v(n, 0, 64)
+    def od(n): return v(n, 64, 128)
+
+    def swap(out, src, d, m, md):
+        tt(v(md), v(d), v(m), A.mult)
+        tt(ev(out), ev(src), v(md), A.add)
+        tt(od(out), od(src), v(md), A.subtract)
+
+    def store(src, cm, ps, stage, y, sem, nv):
+        for gg in range(8):
+            o = (T[cm][:, :, gg, :], [(cm, gg, gg + 1, None)], 128, 4, False)
+            if gg < nv:
+                ts(o, v(src), v("gm", gg, gg + 1), A.mult)
+            else:
+                act(o, v(src), scale=v("gm", gg, gg + 1))
+        for b in range(2):
+            for m in range(4):
+                mm(v(ps, 32 * m + b, 32 * m + 32, 2), (T[cm][:, b, :, m::4], [(cm, 0, 8, None)], 128, 4, False), v("sel16"), True, True)
+        act(v(stage), v(ps, 0, 128))
+        dma("s", hbm(y[:]), v(stage), sem, 64)
+
+    dma("s", v("su32"), hbm(T.su[:]), "qsu", 64)
+    dma("a", v("x0s"), hbm(T.x0[:]), "qx", 512)
+    dma("s", v("lab32"), hbm(T.lab[:]), "qlab", 64)
+    dma("s", v("x0c"), hbm(T.x0[:]), "qxc", 512)
+    mset(v("ones"), 1.0); mset(v("pm"), 0.0); mset(v("id32"), 0.0); mset(v("j0"), 0.0)
+    for b in range(2):
+        aff(v("pm", 136 * b + 8, 136 * b + 136), v("ones"), [[-16, 8], [1000, 2], [-2, 8]], A.is_equal, -b, 1)
+    for n in ("wd", "wdn", "wf", "s8f"):
+        mset(v(n), 0.0)
+    act(v("zb"), v("ones"), scale=0.0); act(v("onesb"), v("ones"))
+    act(v("tw", 0, 8), v("ones", 0, 8), scale=0.0); act(v("tw", 1024, 1040), v("ones", 0, 16), scale=0.0)
+    act(v("bb", 2048, 2064), v("ones", 0, 16), scale=0.0)
+    aff(v("id32", 0, 128), v("ones"), [[-1, 128]], A.is_equal, 0, 1)
+    aff(v("gm1"), v("ones", 0, 8), [[-16, 8]], A.is_ge, 0, 1)
+    aff(v("gm"), v("gm1"), [[16, 8]], A.is_ge, 15, -1)
+    act(v("wd", 15, 143, 16), v("gm")); act(v("wdn", 15, 143, 16), v("gm"), scale=-1.0)
+    act(v("idb"), v("id32", 0, 128)); act(v("idn"), v("id32", 0, 128), scale=-1.0)
+    act(v("idm"), v("id32", 0, 128), scale=128.0); act(v("ids"), v("id32", 0, 128), scale=1.0 / 16)
+    aff(v("gm0"), v("ones", 0, 8), [[-16, 8]], A.is_equal, 0, 1)
+    act(v("wf", 15, 143, 16), v("gm0"))
+    aff(v("s8f", 0, 128, p=(0, 8)), v("ones", p=(0, 8)), [[1, 128]], A.is_equal, -15, -16)
+    iota(v("pcol"), [[0, 4]], 0, 1, False)
+    iota(v("v16"), [[16, 64]], 1, 0, True)
+    iota(v("i16"), [[1, 16]], 0, 0, True)
+    for c in range(2):
+        if not PAR["kc"][0]:
+            iota(blk("kc", c), [[0, 512]], 0, 0, True)
+    for c in range(4):
+        iota(blk("bc", c), [[0, 512]], 0, 0, True)
+        iota(blk("xm", c, 516), [[0, 516]], 0, 0, True)
+    aff(v("xm", 16, 2064, 16), v("onesb"), [[-1, 16], [-16, 8]], A.is_equal, 0, 1)
+    copy(v("idh"), v("id32"))
+    ts(v("pand"), v("pcol"), 15, A.bitwise_and)
+    copy(v("s8h", p=(0, 8)), v("s8f", p=(0, 8)))
+    copy(v("pmf"), v("pand"))
+    ts(v("vp1"), v("v16"), v("pmf", 0, 1), A.add)
+    ts(v("vph"), v("vp1"), 1.0 / 2048, A.mult)
+    ts(v("sel16"), v("i16"), v("pmf", 0, 1), A.is_equal)
+
+    copy(v("suf"), v("su32"))
+    for b in range(2):
+        for h in range(2):
+            mm(blk("gs", b, 64), v("pm", 136 * b + 8 - 8 * h, 136 * b + 136 - 8 * h), v("suf", h, 128, 2), h == 0, h == 1)
+    copy(v("ln"), v("gs", 0, 128))
+    exchange("ln", "p1", 0, "ap1")
+    copy(v("si"), v("gs", 0, 128))
+    act(v("sn"), v("gs", 0, 128))
+    ts(v("lo"), v("si"), 1, A.logical_shift_right, 15, A.bitwise_and)
+    ts(v("bq"), v("si"), 1, A.bitwise_and)
+    ts(v("vi"), v("si"), 1, A.logical_shift_right)
+    ts(v("t1"), v("bq"), 1024.0, A.mult)
+    tt(v("qf"), v("t1"), v("vi"), A.add)
+    jwindow("qf", "lw", "e0")
+    copy(v("lq"), v("qf"))
+    exchange("lq", "p2", 1, "ap2")
+    copy(v("lv"), v("vi"))
+    tt(v("dq"), od("qf"), ev("qf"), A.subtract)
+    tt(v("ds"), od("sn"), ev("sn"), A.subtract)
+
+    copy(v("labf"), v("lab32")); copy(v("labh"), v("labf"))
+    dma("s", v("lrow", p=(0, 8)), v("labh"), "qrow", 32)
+    for b in range(2):
+        for i in range(16):
+            mm(blk("e1", b, 64), v("s8h", 15 - i, 143 - i, p=(0, 8)), v("lrow", 2 * i + b, 2048, 32, p=(0, 8)), i == 0, i == 15)
+    act(v("lc"), v("e1", 0, 128))
+    tt(v("eq"), ev("lc"), od("lc"), A.is_equal)
+    ts(v("ee"), v("eq"), -16384.0, A.mult)
+    tt(v("ts"), ev("lc"), od("lc"), A.add)
+    ts(v("ti"), v("ts"), -1.0, A.mult, 8192.0, A.add)
+    ts(v("thi"), v("ti"), 16352, A.bitwise_and); ts(v("tlo"), v("ti"), 31, A.bitwise_and)
+
+    if PAR["s1"]:
+        for h in range(2): gather_o("og", "x0s", "ln", h)
+        first_sums(0, "a1", "ln", True)
+    for c in range(4):
+        if not PAR["s1"]:
+            tt(blk("a1", c), ind("x0s", "ln", 32 * c, 32 * c + 32), own_x(0, c // 2, 512 * (c % 2), 512, True), A.add)
+        dma("s", blk("a1c", c), blk("a1", c), "qc%d" % c, 128)
+    gains(0, "p1", False, PAR["par1"])
+    act(v("gout1"), v("gs", 0, 64))
+    exchange("gout1", "gin1", 0, "ag1")
+    for hf in range(2):
+        kclear(hf); expand16("vph", hf, False)
+    gains(0, "ln", True, PAR["own1"], PAR["s1"])
+    tt(v("gh"), v("gin1"), v("ee"), A.add)
+    keyout(0)
+    jstep("ja", "j0", "lw", "e0"); copy(v("k1"), v("e0", 0, 128))
+    jstep("jb", "ja", "k1", "e1"); copy(v("k2"), v("e1", 0, 128))
+    jstep("ja", "jb", "k2", "e0"); copy(v("k3"), v("e0", 0, 128))
+    astep("ab", "a1", "a1c", "k1", True, -1)
+    astep("aa", "ab", "ac", "k2", True, 0)
+    astep("ab", "aa", "ac", "k3", False, 1)
+    for h in range(2):
+        act(blk("x1n", h, 1024), blk("ab", h, 1024), bias=255.5 - 1.0 / 32, scale=-1.0 / 16)
+        dma("s", blk("x1c", h, 1024), blk("x1n", h, 1024), "qx%d" % h, 256)
+
+    bstep("ba", "key", "lv", True, True)
+    bstep("bb", "ba", "k1", True)
+    bstep("ba", "bb", "k2", True)
+    bstep("bb", "ba", "k3", False)
+    for h in range(2): extract("e1", "bb", h, "wf")
+    gains(1, "p2", False, PAR["par2"])
+    act(v("gout2"), v("gs", 0, 64))
+    exchange("gout2", "gin2", 1, "ag2")
+    for hf in range(2):
+        kclear(hf); expand16("vph", hf, False)
+    gains(1, "lq", True, PAR["own2"])
+
+    def merges(m):
+        ts(v("wv"), v("bi"), 2047, A.bitwise_and)
+        tt(v("eq"), ev("bi"), od("bi"), A.is_equal)
+        tt(v("iq"), ev("wv"), v("vp1"), A.is_equal)
+        tt(v(m), v("iq"), v("eq"), A.mult)
+        copy(v("lt"), v("wv"))
+        tt(v("thb"), v("thi"), v(m), A.mult)
+        tt(v("tlb"), v("tlo"), v(m), A.mult)
+
+    ts(v("bi"), v("e1", 0, 128), 2048.0, A.mult)
+    merges("m1")
+    ts(v("ee"), v("eq"), -16384.0, A.mult)
+    tt(v("gh"), v("gin2"), v("ee"), A.add)
+    keyout(1)
+    swap("qf2", "qf", "dq", "m1", "md")
+    copy(v("lq2"), v("qf2"))
+    copy(v("si"), v("qf2"))
+    ts(v("lo"), v("si"), 15, A.bitwise_and)
+    jwindow("qf2", "lw2", "e0")
+    twindow()
+
+    jstep("ja", "j0", "lw2", "e0"); copy(v("n1"), v("e0", 0, 128))
+    jstep("tg", "tw", "lt", "gs")
+    tt(v("t1"), v("gs", 0, 128), v("lc"), A.add)
+    ts(v("si"), v("t1"), -1.0, A.mult, 8192.0, A.add)
+    tt(v("l1"), v("si"), v("lc"), A.min)
+    ts(v("bq"), v("si"), 1, A.bitwise_and)
+    ts(v("vi"), v("si"), 1, A.logical_shift_right)
+    ts(v("t2"), v("bq"), 1024.0, A.mult)
+    tt(v("t3"), v("t2"), v("vi"), A.add)
+    ts(v("lm"), v("t3"), 2048.0, A.min)
+    tt(v("ts"), ev("l1"), od("l1"), A.min)
+    ts(v("ti"), v("ts"), -1.0, A.mult, 2048.0, A.add)
+    ts(v("thi"), v("ti"), 4080, A.bitwise_and); ts(v("tlo"), v("ti"), 15, A.bitwise_and)
+    jstep("jb", "ja", "n1", "e1"); copy(v("n2"), v("e1", 0, 128))
+    jstep("ja", "jb", "n2", "e0"); copy(v("n3"), v("e0", 0, 128))
+    jstep("jb", "ja", "n3", "e1"); copy(v("n4"), v("e1", 0, 128))
+    if PAR["s2"]:
+        first_sums(1, "aa", "lq2", False)
+    else:
+        astep("aa", "x1n", "x1c", "lq2", True, 2)
+    bstep("ba", "key", "lv", True, True)
+    bstep("bb", "ba", "k1", True)
+    bstep("ba", "bb", "k2", True)
+    bstep("bb", "ba", "k3", False)
+    for h in range(2): extract("d0", "bb", h, "wf")
+    act(v("t2"), v("d0", 0, 128))
+    for h in range(2):
+        act(blk("ba", h, 1024), ind("bb", "lm", 64 * h, 64 * h + 64))
+        extract("d1", "ba", h, "wf")
+    tt(v("t3"), v("d1", 0, 128), v("t2"), A.max)
+    ts(v("bi"), v("t3"), 2048.0, A.mult)
+    merges("m2")
+    twindow()
+    tt(v("iq"), v("m1"), v("m2"), A.add)
+    swap("sf", "sn", "ds", "iq", "md")
+    store("sf", "cm", "d0", "os1", T.ysu, "qy2", 0)
+    jstep("tg", "tw", "lt", "gs")
+    act(v("t1"), v("gs", 0, 128), bias=2048.0, scale=-1.0)
+    tt(v("lf"), v("t1"), v("l1"), A.min)
+    store("lf", "cn", "d1", "os2", T.ylab, "qy3", PAR["cn"])
+    astep("ab", "aa", "ac", "n1", True, 3)
+    astep("aa", "ab", "ac", "n2", True, 4)
+    astep("ab", "aa", "ac", "n3", True, 5)
+    w = 1024 // PAR["nq"]
+    for hf in range(PAR["nq"]):
+        for b in range(2):
+            c = 1024 * b + w * hf
+            tt(v("aa", c, c + w), ind("ab", "n4", c // 16, (c + w) // 16), v("ac", c, c + w), A.add)
+            act(v("yb", c, c + w), v("aa", c, c + w), bias=0.5 - 1.0 / 64, scale=1.0 / 32)
+            o = v("yo", 2 * w * hf + b, 2 * w * (hf + 1), 2)
+            if (2 * hf + b) * w < 512 * PAR["yo"]:
+                act(o, v("yb", c, c + w), bias=255.0, scale=-1.0)
+            else:
+                ts(o, v("yb", c, c + w), -1.0, A.mult, 255.0, A.add)
+        dma("s", hbm(T.yx[:, 2 * w * hf:2 * w * (hf + 1)]), blk("yo", hf, 2 * w), "qo%d" % hf, w // 2)
+
+    if "order" not in ORDER:
+        acc, deps = {}, []
+        for n, o in enumerate(ops):
+            dep = set(o[8])
+            for lst, isw in ((o[2], False), (o[3], True)):
+                for (name, lo, hi, p) in lst:
+                    for (m, l2, h2, p2, w2) in acc.get(name, []):
+                        if name in PS:
+                            if ops[m][0] != o[0] or w2 or isw:
+                                dep.add(m)
+                        elif (w2 or isw) and l2 < hi and lo < h2 and not (p and p2 and len(p) == len(p2) == 3 and p != p2):
+                            dep.add(m)
+            deps.append(dep)
+            for lst, isw in ((o[2], False), (o[3], True)):
+                for (name, lo, hi, p) in lst:
+                    if name in PS and isw:
+                        acc[name] = []
+                    acc.setdefault(name, []).append((n, lo, hi, p, isw))
+        ORDER["order"], ORDER["deps"] = schedule(ops, deps), deps
+    order, deps = ORDER["order"], ORDER["deps"]
+    pos = {k: n for n, k in enumerate(order)}
+    clock = {q: {} for q in eng}
+    snap, waits, need = {}, {}, set()
+    for k in order:
+        q = ops[k][0]
+        waits[k], snap[k] = [], {}
+        if q == "x":
+            continue
+        ck = clock[q]
+        for m in sorted(deps[k], key=lambda m: -pos[m]):
+            src = ops[m][4] or ops[m][0]
+            if src == "sent" or (src == q == "p") or ck.get(src, -1) >= pos[m]:
+                continue
+            waits[k].append(m); need.add(m); ck[src] = pos[m]
+            for s2, m2 in snap[m].items():
+                if ck.get(s2, -1) < m2:
+                    ck[s2] = m2
+        snap[k] = dict(ck)
+    total, count = {}, {}
+    for k in order:
+        o = ops[k]
+        if o[5] == "c" and k in need:
+            total[csem[o[0]]] = count[k] = total.get(csem[o[0]], 0) + 1
+        elif o[5] == "d":
+            total[o[4]] = count[k] = total.get(o[4], 0) + 16
+        elif o[5] == "x":
+            count[k] = len(use)
+    for k in order:
+        q, fn, sem, kind = ops[k][0], ops[k][1], ops[k][4], ops[k][5]
+        if kind == "x":
+            continue
+        for m in waits[k]:
+            eng[q].wait_ge(T.sem[ops[m][4] or csem[ops[m][0]]], count[m])
+        ins = fn(eng[q])
+        if kind == "c" and k in need:
+            ins.then_inc(T.sem[csem[q]], 1)
+        elif kind == "d":
+            ins.then_inc(T.sem[sem], 16)
+    g.wait_ge(T.sem.sent, nsent[0])
+    for s in ["qy2", "qy3"] + ["qo%d" % c for c in range(PAR["nq"])]:
+        g.wait_ge(T.sem[s], 16)

@@ -1,101 +1,73 @@
-from concourse.bass import DstId, RemoteDMATransfer
-from concourse.mybir import dt, AluOpType, AxisListType, ActivationFunctionType
+from concourse.mybir import AluOpType, ActivationFunctionType
 
 F, B, H, I, U = "float32", "bfloat16", "float16", "int32", "uint16"
 SCRATCH = {}
 for _d, _w, _names in [
-    (B, 2048, "x0s x0c x1n x1c og oh yb yo a1 a1c j0 ja jb tg"), (B, 4096, "rr mm"), (B, 1040, "tw"), (B, 2064, "xm"), (H, 2048, "lrow"),
-    (F, 2048, "aa ab ac ba bc"), (F, 2064, "bb"), (F, 1024, "key kc"), (F, 272, "pm"),
-    (B, 128, "onesb zb idb idn idm ids hib lob"), (B, 144, "wd wdn"), (F, 144, "id32 wf s8f"), (H, 144, "idh s8h"),
-    (F, 8, "gm1 gm gm0"), (I, 4, "pcol pand"), (F, 4, "pmf"), (F, 16, "i16 sel16"),
-    (F, 128, "ones suf t1 t2 t3 sn qf qf2 labf lc l1 lf sf os1 os2"), (I, 128, "su32 si vi bq lo lab32 bi wv"), (H, 128, "labh"),
-    (U, 128, "ln lq lv lw lq2 lw2 lt lm p1 p2 k1 k2 k3 n1 n2 n3 n4"),
-    (F, 64, "v16 vp1 dq ds md gout1 gout2 gin1 gin2 eq ee iq m1 m2 ts"), (H, 64, "vph gh"), (I, 64, "ti thi tlo"), (B, 64, "thb tlb"),
+    (B, 2048, "x0s x0c x1n x1c og oh on g2 g3 yb yo j0 ja jb"), (B, 4096, "rr mm"),
+    (F, 2048, "aa ab ac ba bb bc kw gw"),
+    (B, 128, "idb idn idm ids hib lob"), (B, 144, "wd wdn"), (F, 128, "id32 ones key sb sn sf ub lb tb"), (H, 128, "idh suh"),
+    (F, 8, "gm1 gm selj"), (F, 16, "selb"), (I, 4, "pcol pand"), (F, 4, "mg1 mg0"),
+    (I, 256, "su32"), (I, 128, "lo lab32 bi wv"), (F, 256, "tq tp2"),
+    (U, 256, "ln p1 p2"), (U, 128, "lw k1 k2 k3 n0 n1 n2 n3 n4 lf"),
+    (F, 64, "ev ds md gout1 gout2 gin1 gin2 nq d1 t0 bo t1 t2 t3 m1 mn"), (I, 64, "ei"),
 ]:
     for _n in _names.split():
         SCRATCH[_n] = ("sbuf", [128, _w], _d)
-SCRATCH["cm"] = ("sbuf", [128, 2, 8, 64], F)
-SCRATCH["cn"] = ("sbuf", [128, 2, 8, 64], F)
-PS = ["d0", "d1", "d2", "kp0", "kp1", "gs", "e0", "e1"]
-for _n in PS:
-    SCRATCH[_n] = ("psum", [128, 512], F)
-SEMAPHORES = "cv ca cp cg sent ap1 ap2 ag1 ag2 qsu qx qxc qlab qrow qh ql qy2 qy3 qk0 qk1 qx0 qx1".split()
-SEMAPHORES += ["q%s%d" % (_n, _c) for _n in "abco" for _c in range(4)]
+for _n in ("tf0", "tf1", "th0", "th1"):
+    SCRATCH[_n + "2"] = ("sbuf", [128, 17, 8], F if _n[1] == "f" else H)
+    SCRATCH[_n + "4"] = ("sbuf", [128, 35, 4], F if _n[1] == "f" else H)
+for _n in ("zb", "zo"):
+    SCRATCH[_n] = ("sbuf", [128, 8, 32], H)
+for _n in range(8):
+    SCRATCH["ps%d" % _n] = ("psum", [128, 512], F)
+SEMAPHORES = "cv ca cp cg sent ap1 ap2 ag1 ag2".split() + ["q%d" % _c for _c in range(120)]
 A = AluOpType
 AF = ActivationFunctionType
-PAR = dict(cy=1.0e-3, gather=1.56, pe=0.5e-3, fix=0.06, dma=2.0, bw=2.0e5, rem=3.0, first=2.0, hop=0.1, look=0.1,
-           ca=[1, 0, 0, 0, 0, 0, 0, 0], cb=[0] * 6, kc=[1, 1], nq=4, s1=1, s2=1, own1=2, par1=0, own2=1, par2=2, yo=0, cn=4)
-WEIGHT = {4:4,47:21,71:20,113:3,124:10,127:20,135:9,137:28,139:23,151:16,161:11,167:-14,175:-16,181:6,187:-15,191:-7,194:17,200:-15,202:25,203:27,205:8,206:-9,209:14,261:-7,268:-5,269:28,270:10,279:-15,280:-34,286:-24,288:16,290:-3,301:-7,303:-8,305:-3,308:5,309:8,311:4,312:-2,315:9,316:-12,320:-9,322:-7,333:-8,346:-20,347:8,351:7,352:-19,354:3,357:5,378:-22,386:14,395:23,397:-10,399:-3,405:-9,407:10,408:-6,410:13,415:-5,421:-9,422:-1,424:-13,431:8,432:14,440:1,443:5,448:2,450:-8,457:-5,463:4,467:-1,470:-7,477:-11,480:13,487:6,492:-4,494:4,496:-10,498:-5,499:-20,500:6,501:6,503:13,504:-5,505:36,508:-7,511:8,555:1,556:1,574:16,595:2,646:1,663:8,665:4,666:22,701:-18,703:2,704:5,708:4,709:-3,714:2,715:6,718:-7,732:18,735:-16,736:3,737:-9,738:4,744:-3,745:13,748:-8,753:-10,755:-7,757:-15,759:1,766:-11,770:-6,773:-4,776:12,777:-12,778:16,779:-4,780:-5,781:13,793:2,794:2,795:20,797:6,798:2,800:2,802:7,803:4,804:-16,807:1,809:4,811:13,814:4,815:-3,816:7,817:-3,819:12,820:10,822:13,824:10,825:-4,826:1,827:-2,828:-5,830:8,833:-8,836:18,837:-2,839:-2,840:14,841:-2,842:-5,843:-5,844:2,845:-3,846:21,847:3,848:11,849:3,851:-12,856:-20,857:-6,862:-34,882:-16,887:-29,899:-7,933:-25,934:27,978:5,986:-14,988:29,991:15,998:14,1007:26,1083:-10,1084:5,1159:-24,1160:-30,1164:-6,1167:-7,1170:12,1182:3,1215:3,1216:2,1217:-2,1222:1,1223:3,1224:5,1225:9,1233:-4,1234:2,1235:1,1238:1,1239:12,1246:2,1251:-9,1254:3,1255:4,1257:-14,1260:-12,1263:-8,1264:-10,1265:8,1268:-10,1269:-1,1270:-20,1274:-2,1279:-18,1280:3,1283:-9,1285:-7,1287:-19}
-ORDER = {}
+PAR = dict(cy=0.85e-3, gather=1.56, pe=0.43e-3, fix=0.06, dma=1.9, bw=4.0e5, rem=3.0, first=2.0, hop=0.08)
+SPLIT = {'own1': 'gggg', 'par1': 'ffgg', 'own2': 'gggg', 'par2': 'gggg', 'og1': 'av', 'pg1': 'aa', 'og2': 'aa', 'on2': 'aa', 'pg2': 'aa', 'or1': 'vvaaaaaa', 'pr1': 'aaaaaaaa', 'or2': 'aaaaaaaa', 'pr2': 'aaaaaaaa', 'fs1': 'aaaa', 'fs2': 'aaaa', 'j1': 'vvaaaa', 'a12': 'vvvv', 'a13': 'vvvv', 'a22': 'aavv', 'a23': 'aavv', 'jq': 2, 'je': 'a', 'fin': 'aaaa', 'lg': 'av', 'zero': 'g', 'te': 'aa', 'new2': 0, 'ride': 0, 'b14': 'vvvv', 'b25': 'vaaa', 'a14': 'vvvv', 'a24': 'vvvv', 'a25': 'vvvv', 'ko': 'aaa'}
+SEQ = '31 2 38 1 0 39 3 8 5 6 9 7 10 20 16 23 15 19 4 17 22 30 18 24 40 53 41 54 46 25 42 43 26 47 63 49 48 64 51 50 92 55 56 95 93 27 60 11 28 98 52 12 96 94 57 21 131 115 34 13 99 89 97 119 90 35 100 121 134 116 132 91 122 33 113 65 133 135 71 29 136 185 120 107 76 32 140 74 189 186 80 36 82 66 190 81 101 58 44 45 141 37 83 183 68 75 103 142 184 59 137 109 70 187 14 138 67 114 188 77 139 69 61 193 146 72 73 78 79 197 194 84 85 108 102 147 198 86 195 105 143 87 88 191 196 104 110 192 144 148 106 145 202 111 112 117 118 200 123 124 125 126 127 199 128 130 129 201 62 204 149 203 219 151 150 223 217 155 152 207 224 153 156 232 205 225 154 157 211 213 212 159 158 240 208 163 236 160 206 161 214 234 164 209 210 233 215 162 165 216 167 166 218 246 171 168 226 248 220 252 169 172 241 242 170 173 247 221 222 227 237 228 174 177 229 235 230 231 254 176 249 178 255 175 238 239 253 244 179 243 180 245 181 182 250 258 251 259 260 256 261 257 262 263 273 264 274 265 267 266 275 268 276 269 277 279 270 278 272 271 284 292 287 290 293 288 280 296 298 291 289 294 297 282 299 285 300 295 302 281 301 286 308 283 306 303 309 392 304 305 314 307 395 310 312 396 311 315 316 398 397 313 393 317 318 399 400 394 322 401 319 402 320 321 323 324 403 326 325 330 404 328 327 405 331 406 410 332 329 334 333 411 338 407 335 340 339 336 408 355 337 412 343 409 341 413 356 344 357 342 345 418 347 346 419 414 352 358 351 415 348 349 350 360 416 353 361 420 417 354 362 421 424 359 363 366 430 364 367 422 365 369 431 368 426 371 370 376 427 372 383 373 377 374 378 375 379 423 380 428 425 381 429 384 432 382 385 388 386 433 390 387 389 391'
+BK = '1005602623463245157023777135552760431727346016213064572605326413726541031470'
 
 
-def place(ops, pred, succ, prio, back=False):
-    n = len(ops)
-    left = [len(p) for p in pred]
-    est = [0.0] * n
-    ready = {q: [] for q in "vapgsx"}
-    free = {q: 0.0 for q in "vapgsx"}
-    for k in range(n):
-        if not left[k]:
-            ready[ops[k][0]].append(k)
-    order = []
-    while len(order) < n:
-        best = None
-        for q in ready:
-            if ready[q]:
-                t0 = max(free[q], min(est[k] for k in ready[q]))
-                if best is None or t0 < best[0]:
-                    best = (t0, q)
-        t0, q = best
-        k = max((k for k in ready[q] if est[k] <= t0 + PAR["look"]), key=lambda k: (prio[k], -k))
-        ready[q].remove(k)
-        st = max(free[q], est[k])
-        free[q] = st + ops[k][7]
-        order.append(k)
-        for s in succ[k]:
-            est[s] = max(est[s], st + ops[k][6] + (0.0 if ops[s][0] == q == "p" else PAR["hop"]))
-            left[s] -= 1
-            if not left[s]:
-                ready[ops[s][0]].append(s)
-    return (order,)
-
-
-def schedule(ops, deps):
-    n = len(ops)
-    succ = [[] for _ in range(n)]
-    for k in range(n):
-        for m in deps[k]:
-            succ[m].append(k)
-    pr = [0.0] * n
-    for k in range(n - 1, -1, -1):
-        pr[k] = ops[k][6] + WEIGHT.get(k, 0) + max([pr[s] + 0.1 for s in succ[k]] + [0.0])
-    return place(ops, deps, succ, pr)[0]
-
-
-def rank_program(g, core, T, topo):
+def record(core, T, topo, banks):
     rank = T.rank_of(core)
-    if rank is None:
-        return
-    eng = {"v": g.vector, "a": g.scalar, "p": g.tensor, "g": g, "s": g.sync}
-    csem = {"v": "cv", "a": "ca", "p": "cp", "g": "cg"}
     ops = []
-    cy, fix = PAR["cy"], PAR["fix"]
+    cy, fix, S = PAR["cy"], PAR["fix"], SPLIT
     size = {F: 4, B: 2, H: 2, I: 4, U: 2}
+    ALL = (1 << 128) - 1
+    part = ["c"]
+
+    def at(name): part[0] = name
 
     def v(name, a=None, b=None, s=None, p=None):
-        w = SCRATCH[name][1][1]
+        real = "ps%d" % banks.get(name, 0) if name[0] == "#" else name
+        w = SCRATCH[real][1][1]
         a = 0 if a is None else a
         b = w if b is None else b
         ps = slice(None) if p is None else slice(p[0], p[1], p[2] if len(p) > 2 else None)
-        return (T[name][ps, a:b:s] if s else T[name][ps, a:b], [(name, a, b, p)], len(range(a, b, s or 1)), size[SCRATCH[name][2]], name in PS)
+        pm = ALL if p is None else sum(1 << x for x in range(128)[ps])
+        return (T[real][ps, a:b:s] if s else T[real][ps, a:b], [(name, a, b, pm)], len(range(a, b, s or 1)), size[SCRATCH[real][2]], name[0] == "#")
 
     def blk(name, c, n=512, p=None): return v(name, n * c, n * c + n, p=p)
+    def ev(n): return v(n, 0, 128, 2)
+    def od(n): return v(n, 1, 128, 2)
+
+    def z(name, half=None, u=None):
+        if half is None:
+            return (T[name][:], [(name, 0, 32, ALL)], 256, 2, False)
+        if u is None:
+            return (T[name][:, :, 16 * half:16 * half + 16], [(name, 16 * half, 16 * half + 16, ALL)], 128, 2, False)
+        return (T[name][:, u, 16 * half:16 * half + 16], [(name, 16 * half, 16 * half + 16, ALL)], 16, 2, False)
+
+    def y(name, a, b, s=1):
+        name += str(S["jq"])
+        return (T[name][:, a:b:s, :], [(name, 0, 35, ALL)], 16 // S["jq"] * len(range(a, b, s)), size[SCRATCH[name][2]], False)
 
     def ind(win, lst, c, d):
-        return (T[win][:, 0:SCRATCH[win][1][1]].indirect(T[lst][:, c:d]), [(win, 0, 1 << 20, None), (lst, c, d, None)], 16 * (d - c), 4, "ind")
+        return (T[win][:, 0:SCRATCH[win][1][1]].indirect(T[lst][:, c:d]), [(win, 0, 1 << 20, ALL), (lst, c, d, ALL)], 16 * (d - c), 4, "ind")
 
     def rec(q, fn, reads, writes, lat, sem=None, kind="c", busy=None, after=()):
-        ops.append([q, fn, sum([r[1] for r in reads], []), sum([w[1] for w in writes], []), sem, kind, lat, lat if busy is None else busy, list(after)])
+        ops.append([q, fn, sum([r[1] for r in reads], []), sum([w[1] for w in writes], []), sem, kind, lat, lat if busy is None else busy, list(after), part[0]])
         return len(ops) - 1
 
     def cost(o, i, mult=1.0, half=True):
@@ -108,6 +80,7 @@ def rank_program(g, core, T, topo):
     def copy(o, i): rec("v", lambda e: e.tensor_copy(o[0], i[0]), [i], [o], cost(o, i))
     def tt(o, a, b, op): rec("v", lambda e: e.tensor_tensor(o[0], a[0], b[0], op), [a, b], [o], cost(o, a, 1 if a[4] or b[4] else 2, False))
     def mset(o, c): rec("v", lambda e: e.memset(o[0], c), [], [o], cost(o, o))
+    def turn(o, i): rec("v", lambda e: e.transpose(o[0], i[0]), [i], [o], cost(o, i))
 
     def ts(o, a, s1, op0, s2=None, op1=None):
         rd = [a] + [s for s in (s1, s2) if isinstance(s, tuple)]
@@ -119,12 +92,32 @@ def rank_program(g, core, T, topo):
 
     def act(o, i, func=None, bias=0.0, scale=1.0):
         f = AF.Identity if func is None else func
-        rd = [i] + ([scale] if isinstance(scale, tuple) else [])
-        sc = scale[0] if isinstance(scale, tuple) else scale
-        rec("a", lambda e: e.activation(o[0], i[0], f, bias=bias, scale=sc), rd, [o], cost(o, i, 1, False))
+        rec("a", lambda e: e.activation(o[0], i[0], f, bias=bias, scale=scale), [i], [o], cost(o, i, 1, False))
+
+    def lin(q, o, i, bias=0.0, scale=1.0):
+        if q == "a":
+            act(o, i, None, bias, scale)
+        elif bias == 0.0 and scale == 1.0:
+            copy(o, i)
+        else:
+            ts(o, i, scale, A.mult, bias, A.add)
+
+    def relu(q, o, i):
+        if q == "a":
+            act(o, i, AF.Relu)
+        else:
+            ts(o, i, 0.0, A.max)
 
     def mm(o, l, r, st, sp):
         rec("p", lambda e: e.matmul(o[0], l[0], r[0], st, sp), [l, r], [o], max(min(64, l[2]), r[2]) * l[3] * l[3] / 4 * PAR["pe"])
+
+    def mms(calls):
+        def fn(e):
+            for (o, l, r, st, sp) in calls:
+                ins = e.matmul(o[0], l[0], r[0], st, sp)
+            return ins
+        rec("p", fn, sum([[c[1], c[2]] for c in calls], []), [c[0] for c in calls],
+            sum(max(min(64, l[2]), r[2]) * l[3] * l[3] / 4 * PAR["pe"] for (o, l, r, st, sp) in calls))
 
     def aff(o, i, pat, cmp, base, cm): rec("g", lambda e: e.affine_select(o[0], i[0], pat, cmp, 0.0, base, cm), [i], [o], 0.17 + 2 * o[2] * cy)
 
@@ -134,359 +127,402 @@ def rank_program(g, core, T, topo):
         else:
             rec("g", lambda e: e.iota(o[0], pat, base, cm), [], [o], 0.13 + 2 * o[2] * cy)
 
-    def dma(q, o, i, sem, kb):
+    nq, nb = [0], [0]
+
+    def dma(q, o, i, kb):
         t = kb * 1024 / PAR["bw"]
-        rec(q, lambda e: e.dma_start(o[0], i[0]), [i], [o], PAR["dma"] + t, sem, "d", max(0.1, t) if q == "s" else 0.1)
+        nq[0] += 1
+        rec(q, lambda e: e.dma_start(o[0], i[0]), [i], [o], PAR["dma"] + t, "q%d" % (nq[0] - 1), "d", max(0.1, t) if q == "s" else 0.1)
+
+    def bank():
+        nb[0] += 1
+        return "#%d" % nb[0]
 
     def hbm(ap): return (ap, [])
-    ROW = (0, 128, 16)
+    ROW, JROW, LROW, BL = (0, 128, 16), (1, 128, 16), (8, 128, 16), (0, 128, 8)
 
     pa = [T.cores[rank ^ 1], T.cores[rank ^ 2]]
     use = [e for e in topo.engines(core, pa[0]) if e in topo.engines(core, pa[1])][:8]
     emask = sum(1 << e for e in use)
     nsent = [0]
 
-    def exchange(src, dst, r, sem):
+    def exchange(src, dst, r, sem, w=None):
         rid, pid, _se = topo.addr(pa[r])
         ex = 0.0 if nsent[0] else PAR["first"]
         nsent[0] += len(use)
-        k = rec("g", lambda e: e.remote_dma(T[dst][:], T[src][:], T.sem[sem], T.sem.sent, pid, rid, emask), [v(src)], [], PAR["rem"] + ex, "sent", "r", 0.5 + ex)
-        rec("x", None, [], [v(dst)], 0.0, sem, "x", after=[k])
+        s_, d_ = v(src, 0, w), v(dst, 0, w)
+        k = rec("g", lambda e: e.remote_dma(d_[0], s_[0], T.sem[sem], T.sem.sent, pid, rid, emask), [s_], [], PAR["rem"] + ex, "sent", "r", 0.5 + ex)
+        rec("x", None, [], [d_], 0.0, sem, "x", after=[k])
 
-    def extract(ps, src, h, mask="wd"):
-        for i in range(16):
-            mm(blk(ps, h, 64), v(mask, 15 - i, 143 - i), v(src, 1024 * h + i, 1024 * (h + 1), 16), i == 0, i == 15)
+    def to_list(src, dst):
+        ts(z("zb", 0), src, v("mg0", 0, 1), A.mult)
+        ts(z("zb", 1), src, v("mg1", 0, 1), A.mult)
+        turn(z("zo"), z("zb"))
+        ps = bank()
+        mms([(v(ps, u, 128, 8), v("idh"), z("zo", h, u), h == 0, h == 1) for u in range(8) for h in range(2)])
+        copy(v(dst), v(ps, 0, 128))
 
-    def jstep(out, win, lst, ps):
+    def turned(src, n):
+        ps = bank()
+        for c in range(4):
+            mms([(v(ps, k, 128 * n, 16), v(src, 128 * k, 128 * k + 128), v("selb", 0, 8 * n), True, True) for k in range(4 * c, 4 * c + 4)])
+        return ps
+
+    def to_block(src, n, q, prev=None):
+        if prev:
+            act(v("tq", 0, 128 * n), v(turned(prev, n), 0, 128 * n))
+        ps, out = turned(src, n), []
+        for r in range(n):
+            out.append(bank())
+            if prev:
+                tt(blk("tp2", r, 128), blk(ps, r, 128), blk("tq", r, 128), A.max)
+            else:
+                lin(q, blk("tp2", r, 128), blk(ps, r, 128))
+            mm(v(out[r], 0, 128), blk("tp2", r, 128), v("id32"), True, True)
+        return [v(o, 0, 128) for o in out]
+
+    def jlist(src, dst):
+        n = S["jq"]
+        m, r = 128 // n, 16 // n
+        for c in range(n):
+            ps, p2 = bank(), bank()
+            tp, idm = ("tf%d" % (c % 2), "id32") if S["je"] == "a" else ("th%d" % (c % 2), "idh")
+            mms([(v(ps, i, 8 * r, r), v(src, 16 * m * c + i, 16 * m * (c + 1), r), v("selj"), True, True) for i in range(r)])
+            lin(S["je"], y(tp, n - 1, 9 * n - 1, n), v(ps, 0, 8 * r))
+            mms([(v(p2, 0, m), y(tp, n - 1 - b, 9 * n - 1 - b), v(idm, b, 128, n), b == 0, b == n - 1) for b in range(n)])
+            copy(v(dst, m * c, m * (c + 1)), v(p2, 0, m))
+
+    def jstep(out, win, lst, dst, who):
         for h in range(2):
-            act(blk(out, h, 1024), ind(win, lst, 64 * h, 64 * h + 64))
-            extract(ps, out, h)
+            ps = bank()
+            lin(who[h], blk(out, h, 1024), ind(win, lst, 64 * h, 64 * h + 64))
+            mms([(v(ps, 0, 64), v("wd", 15 - i, 143 - i), v(out, 1024 * h + i, 1024 * (h + 1), 16), i == 0, i == 15) for i in range(16)])
+            copy(blk(dst, h, 64), v(ps, 0, 64))
 
-    def second(out, c, step):
-        if c >= 4 - PAR["ca"][step]:
-            act(blk("ac", c), blk(out, c))
-        else:
-            dma("s", blk("ac", c), blk(out, c), "qa%d" % c, 256)
-
-    def astep(out, win, in1, lst, keep, step):
+    def bstep(out, win, lst, keep, rows, who="vvvv"):
         for c in range(4):
-            tt(blk(out, c), ind(win, lst, 32 * c, 32 * c + 32), blk(in1, c), A.add)
-            if keep:
-                second(out, c, step)
+            if who[c] == "v":
+                tt(blk(out, c), ind(win, lst, 32 * c, 32 * c + 32), blk("bc", c), A.max)
+            else:
+                act(blk(out, c), ind(win, lst, 32 * c, 32 * c + 32))
+            if keep[c] == "v":
+                dma("s", blk("bc", c, p=rows), blk(out, c, p=rows), 16 * 16 // rows[2])
 
-    def bstep(out, win, lst, keep, first=False):
+    def first_sums(x, og, who, bias, nxt):
         for c in range(4):
-            tt(blk(out, c), ind(win, lst, 32 * c, 32 * c + 32), blk("kc", c % 2) if first else blk("bc", c), A.max)
-            if keep and c >= 4 - PAR["cb"][nb[0]]:
-                act(blk("bc", c), blk(out, c))
-            elif keep:
-                dma("s", blk("bc", c, p=ROW), blk(out, c, p=ROW), "qb%d" % c, 16)
-        nb[0] += 1 if keep else 0
-
-    TERMS = [(0, 0, "wd"), (1, 0, "wdn"), (1, 1, "wd"), (0, 1, "wdn")]
-    dn, nb = [0], [0]
-
-    def bank():
-        dn[0] += 1
-        return "d%d" % (dn[0] % 3)
-
-    def own_x(r, b, a, n, sec=False):
-        if r == 0:
-            return v("x0c" if sec else "x0s", 2 * a + b, 2 * (a + n), 2)
-        return v("x1c" if sec else "x1n", 1024 * b + a, 1024 * b + a + n)
-
-    def gather_o(og, win, lst, h): act(blk(og, h, 1024), ind(win, lst, 64 * h, 64 * h + 64))
-
-    def gains(r, lst, own, nact, gathered=False):
-        rr, og, win = ("rr" if own else "mm"), ("og" if own else "oh"), ("x0s", "x1n")[r]
-        for k in range(4):
-            b, h, mask = TERMS[k]
-            if h < nact and k % 2 == 0 and not gathered:
-                gather_o(og, win, lst, h)
-            for hf in range(2):
-                o = blk(rr, 2 * k + hf)
-                if h < nact:
-                    d = bank()
-                    mm(v(d), v("idb"), own_x(r, b, 512 * hf, 512), True, False)
-                    mm(v(d), v("idn"), blk(og, 2 * h + hf), False, True)
-                    act(o, v(d), AF.Relu)
-                else:
-                    tt(o, ind(win, lst, 64 * h + 32 * hf, 64 * h + 32 * hf + 32), own_x(r, b, 512 * hf, 512, True), A.max)
-                if own:
-                    mm(v("kp%d" % hf), v(mask, 15, 143), o, False, False)
-            if not own:
-                for i in range(16):
-                    mm(v("gs", 0, 64), v(mask, 15 - i, 143 - i), v(rr, 1024 * k + i, 1024 * (k + 1), 16), k == 0 and i == 0, k == 3 and i == 15)
-
-    def first_sums(r, out, lst, gathered):
-        for c in range(4):
-            if c % 2 == 0 and not gathered:
-                gather_o("og", "x1n", lst, c // 2)
             d = bank()
-            mm(v(d), v("idb"), own_x(r, c // 2, 512 * (c % 2), 512), True, False)
-            mm(v(d), v("idb"), blk("og", c), False, True)
-            act(blk(out, c), v(d))
-            if r:
-                second(out, c, 2)
+            mms([(v(d), v("idb"), blk(x, c), True, False), (v(d), v("idb"), blk(og, c), False, True)])
+            lin(who[c], blk("aa", c), v(d), bias)
+            if nxt[c] == "v":
+                dma("s", blk("ac", c), blk("aa", c), 256)
 
-    def kclear(hf): mm(v("kp%d" % hf), v("zb"), v("x0s", 0, 512), True, False)
-
-    def expand16(src, hf, last):
-        for i in range(16):
-            mm(v("kp%d" % hf, i, 512, 16), v("idh", i, i + 128), blk(src, hf, 32), False, last and i == 15)
-
-    def keyout(r):
-        for hf in range(2):
-            expand16("gh", hf, True)
-            act(blk("key", hf), v("kp%d" % hf), AF.Relu, bias=4096.0)
-            if PAR["kc"][r]:
-                act(blk("kc", hf), v("kp%d" % hf), AF.Relu, bias=4096.0)
+    def astep(out, win, lst, who, nxt, parts=(), gbias=0.0, bias=0.0):
+        for c in range(4):
+            if who[c] == "v":
+                tt(blk(out, c), ind(win, lst, 32 * c, 32 * c + 32), blk("ac", c), A.add)
+            elif who[c] == "w":
+                act(blk("gw", c), ind(win, lst, 32 * c, 32 * c + 32))
+                d = bank()
+                mms([(v(d), v("id32"), blk(win, c), True, False), (v(d), v("id32"), blk("gw", c), False, True)])
+                act(blk(out, c), v(d))
             else:
-                dma("s", blk("kc", hf, p=ROW), blk("key", hf, p=ROW), "qk%d" % hf, 16)
+                act(blk(parts[-1], c), ind(win, lst, 32 * c, 32 * c + 32), None, gbias)
+                d = bank()
+                mms([(v(d), v("idb"), blk(s_, c), n == 0, n == len(parts) - 1) for n, s_ in enumerate(parts)])
+                lin("a" if who[c] == "a" else "v", blk(out, c), v(d), bias)
+            if nxt[c] == "v":
+                dma("s", blk("ac", c), blk(out, c), 256)
 
-    def twindow():
-        for hf in range(2):
-            kclear(hf)
-            for r, src in ((0, "thb"), (1, "tlb")):
-                for i in range(16):
-                    mm(v("kp%d" % hf, i, 512, 16), v("xm", 16 - r + 128 * i, 144 - r + 128 * i), blk(src, hf, 32), False, r == 1 and i == 15)
-            act(v("tw", 1 + 512 * hf, 513 + 512 * hf), v("kp%d" % hf))
+    def sums(r, x, og, lists, s2, s3, s4, off, unit, beta):
+        at("a2" + r)
+        astep("ab", "aa", lists[0], s2, s3, [x, og, "g2"], -beta, 2 * beta - 2 * off)
+        at("a3" + r)
+        astep("aa", "ab", lists[1], s3, s4, [x, og, "g2", "g3"], -2 * beta - 256 * unit, 4 * beta - 2 * off + 256 * unit)
 
-    def jwindow(q, lw, ps):
-        ts(v("lob"), v("lo"), 1.0, A.mult)
-        dma("s", v("j0", p=(1, 128, 16)), v("lob"), "ql", 32)
-        tt(v("hib"), v(q), v("lo"), A.subtract)
-        dma("s", v("j0", p=ROW), v("hib"), "qh", 32)
-        mm(v(ps, 0, 128), v("idm"), v("lob"), True, False)
-        mm(v(ps, 0, 128), v("ids"), v("hib"), False, True)
-        copy(v(lw), v(ps, 0, 128))
+    def gather(og, x, lst, who, kind="gggg"):
+        for h in range(2):
+            a = 2 * h + (kind[2 * h] != "g")
+            b = 2 * h + 1 + (kind[2 * h + 1] == "g")
+            if a < b:
+                lin(who[h], v(og, 512 * a, 512 * b), ind(x, lst, 32 * a, 32 * b))
 
-    def ev(n): return v(n, 0, 64)
-    def od(n): return v(n, 64, 128)
-
-    def swap(out, src, d, m, md):
-        tt(v(md), v(d), v(m), A.mult)
-        tt(ev(out), ev(src), v(md), A.add)
-        tt(od(out), od(src), v(md), A.subtract)
-
-    def store(src, cm, ps, stage, y, sem, nv):
-        for gg in range(8):
-            o = (T[cm][:, :, gg, :], [(cm, gg, gg + 1, None)], 128, 4, False)
-            if gg < nv:
-                ts(o, v(src), v("gm", gg, gg + 1), A.mult)
+    def gains(x, xc, lst, lsw, og, rr, kind, who):
+        ps = bank()
+        for c in range(4):
+            if kind[c] == "f":
+                tt(blk(rr, c), ind(x, lst, 32 * c, 32 * c + 32), blk(xc, c), A.max)
+                tt(blk(rr, 4 + c), ind(x, lsw[0], lsw[1] + 32 * c, lsw[1] + 32 * c + 32), blk(xc, c), A.max)
             else:
-                act(o, v(src), scale=v("gm", gg, gg + 1))
-        for b in range(2):
-            for m in range(4):
-                mm(v(ps, 32 * m + b, 32 * m + 32, 2), (T[cm][:, b, :, m::4], [(cm, 0, 8, None)], 128, 4, False), v("sel16"), True, True)
-        act(v(stage), v(ps, 0, 128))
-        dma("s", hbm(y[:]), v(stage), sem, 64)
+                d = bank()
+                mms([(v(d), v("idb"), blk(x, c), True, False), (v(d), v("idn"), blk(og, c), False, True)])
+                relu(who[2 * c], blk(rr, c), v(d))
+                d = bank()
+                mms([(v(d), v("idb"), blk(x, c), True, False),
+                     (v(d, 0, 512, 2), v("idn"), v(og, 512 * c + 1, 512 * c + 512, 2), False, False),
+                     (v(d, 1, 512, 2), v("idn"), v(og, 512 * c, 512 * c + 512, 2), False, True)])
+                relu(who[2 * c + 1], blk(rr, 4 + c), v(d))
+            for t, mask in ((0, "wd"), (1, "wdn")):
+                mms([(v(ps, 0, 64), v(mask, 15 - k, 143 - k), v(rr, 2048 * t + 128 * k + b, 2048 * t + 128 * k + 128, 2),
+                      (c, t, k, b) == (0, 0, 0, 0), (c, t, k, b) == (3, 1, 15, 1)) for k in range(4 * c, 4 * c + 4) for b in range(2)])
+        return v(ps, 0, 64)
 
-    dma("s", v("su32"), hbm(T.su[:]), "qsu", 64)
-    dma("a", v("x0s"), hbm(T.x0[:]), "qx", 512)
-    dma("s", v("lab32"), hbm(T.lab[:]), "qlab", 64)
-    dma("s", v("x0c"), hbm(T.x0[:]), "qxc", 512)
-    mset(v("ones"), 1.0); mset(v("pm"), 0.0); mset(v("id32"), 0.0); mset(v("j0"), 0.0)
-    for b in range(2):
-        aff(v("pm", 136 * b + 8, 136 * b + 136), v("ones"), [[-16, 8], [1000, 2], [-2, 8]], A.is_equal, -b, 1)
-    for n in ("wd", "wdn", "wf", "s8f"):
+    def keys(side):
+        tt(v("t2"), v("t1"), v("nq"), A.mult)
+        tt(ev("key"), v("t2"), v("ev"), A.add)
+        lin(S["ko"][side], od("key"), ev("key"), float(side))
+        dma("s", v("kw", p=ROW), v("key"), 64)
+        dma("s", v("bc", p=ROW), v("key"), 64)
+
+    def swap(out, src, m, d):
+        tt(v("md"), v(d), v(m), A.mult)
+        tt(ev(out), ev(src), v("md"), A.add)
+        tt(od(out), od(src), v("md"), A.subtract)
+
+    f1, f2 = "f" in S["par1"] + S["own1"], "f" in S["par2"] + S["own2"]
+    at("ld")
+    dma("s", v("su32", 0, 128), hbm(T.su[:]), 64)
+    dma("a", v("x0s"), hbm(T.x0[:]), 512)
+    at("ld2")
+    if f1 or f2:
+        dma("s", v("su32", 128, 256, p=(0, 128, 2)), hbm(T.su[1:128:2, :]), 32)
+        dma("s", v("su32", 128, 256, p=(1, 128, 2)), hbm(T.su[0:128:2, :]), 32)
+    at("ld3")
+    dma("s", v("lab32"), hbm(T.lab[:]), 64)
+    if f1:
+        dma("s", v("x0c"), hbm(T.x0[:]), 512)
+    at("c1")
+    mset(v("ones"), 1.0); mset(v("j0"), 0.0)
+    for n in ("wd", "wdn"):
         mset(v(n), 0.0)
-    act(v("zb"), v("ones"), scale=0.0); act(v("onesb"), v("ones"))
-    act(v("tw", 0, 8), v("ones", 0, 8), scale=0.0); act(v("tw", 1024, 1040), v("ones", 0, 16), scale=0.0)
-    act(v("bb", 2048, 2064), v("ones", 0, 16), scale=0.0)
-    aff(v("id32", 0, 128), v("ones"), [[-1, 128]], A.is_equal, 0, 1)
+    aff(v("id32"), v("ones"), [[-1, 128]], A.is_equal, 0, 1)
     aff(v("gm1"), v("ones", 0, 8), [[-16, 8]], A.is_ge, 0, 1)
     aff(v("gm"), v("gm1"), [[16, 8]], A.is_ge, 15, -1)
     act(v("wd", 15, 143, 16), v("gm")); act(v("wdn", 15, 143, 16), v("gm"), scale=-1.0)
-    act(v("idb"), v("id32", 0, 128)); act(v("idn"), v("id32", 0, 128), scale=-1.0)
-    act(v("idm"), v("id32", 0, 128), scale=128.0); act(v("ids"), v("id32", 0, 128), scale=1.0 / 16)
-    aff(v("gm0"), v("ones", 0, 8), [[-16, 8]], A.is_equal, 0, 1)
-    act(v("wf", 15, 143, 16), v("gm0"))
-    aff(v("s8f", 0, 128, p=(0, 8)), v("ones", p=(0, 8)), [[1, 128]], A.is_equal, -15, -16)
-    iota(v("pcol"), [[0, 4]], 0, 1, False)
-    iota(v("v16"), [[16, 64]], 1, 0, True)
-    iota(v("i16"), [[1, 16]], 0, 0, True)
-    for c in range(2):
-        if not PAR["kc"][0]:
-            iota(blk("kc", c), [[0, 512]], 0, 0, True)
-    for c in range(4):
-        iota(blk("bc", c), [[0, 512]], 0, 0, True)
-        iota(blk("xm", c, 516), [[0, 516]], 0, 0, True)
-    aff(v("xm", 16, 2064, 16), v("onesb"), [[-1, 16], [-16, 8]], A.is_equal, 0, 1)
+    act(v("idb"), v("id32")); act(v("idn"), v("id32"), scale=-1.0)
+    act(v("idm"), v("id32"), scale=128.0); act(v("ids"), v("id32"), scale=1.0 / 16)
     copy(v("idh"), v("id32"))
-    ts(v("pand"), v("pcol"), 15, A.bitwise_and)
-    copy(v("s8h", p=(0, 8)), v("s8f", p=(0, 8)))
-    copy(v("pmf"), v("pand"))
-    ts(v("vp1"), v("v16"), v("pmf", 0, 1), A.add)
-    ts(v("vph"), v("vp1"), 1.0 / 2048, A.mult)
-    ts(v("sel16"), v("i16"), v("pmf", 0, 1), A.is_equal)
-
-    copy(v("suf"), v("su32"))
-    for b in range(2):
-        for h in range(2):
-            mm(blk("gs", b, 64), v("pm", 136 * b + 8 - 8 * h, 136 * b + 136 - 8 * h), v("suf", h, 128, 2), h == 0, h == 1)
-    copy(v("ln"), v("gs", 0, 128))
-    exchange("ln", "p1", 0, "ap1")
-    copy(v("si"), v("gs", 0, 128))
-    act(v("sn"), v("gs", 0, 128))
-    ts(v("lo"), v("si"), 1, A.logical_shift_right, 15, A.bitwise_and)
-    ts(v("bq"), v("si"), 1, A.bitwise_and)
-    ts(v("vi"), v("si"), 1, A.logical_shift_right)
-    ts(v("t1"), v("bq"), 1024.0, A.mult)
-    tt(v("qf"), v("t1"), v("vi"), A.add)
-    jwindow("qf", "lw", "e0")
-    copy(v("lq"), v("qf"))
-    exchange("lq", "p2", 1, "ap2")
-    copy(v("lv"), v("vi"))
-    tt(v("dq"), od("qf"), ev("qf"), A.subtract)
-    tt(v("ds"), od("sn"), ev("sn"), A.subtract)
-
-    copy(v("labf"), v("lab32")); copy(v("labh"), v("labf"))
-    dma("s", v("lrow", p=(0, 8)), v("labh"), "qrow", 32)
-    for b in range(2):
-        for i in range(16):
-            mm(blk("e1", b, 64), v("s8h", 15 - i, 143 - i, p=(0, 8)), v("lrow", 2 * i + b, 2048, 32, p=(0, 8)), i == 0, i == 15)
-    act(v("lc"), v("e1", 0, 128))
-    tt(v("eq"), ev("lc"), od("lc"), A.is_equal)
-    ts(v("ee"), v("eq"), -16384.0, A.mult)
-    tt(v("ts"), ev("lc"), od("lc"), A.add)
-    ts(v("ti"), v("ts"), -1.0, A.mult, 8192.0, A.add)
-    ts(v("thi"), v("ti"), 16352, A.bitwise_and); ts(v("tlo"), v("ti"), 31, A.bitwise_and)
-
-    if PAR["s1"]:
-        for h in range(2): gather_o("og", "x0s", "ln", h)
-        first_sums(0, "a1", "ln", True)
+    at("c2")
+    aff(v("selb"), v("ones", 0, 16), [[-8, 2], [-16, 8]], A.is_equal, 0, 1)
+    aff(v("selj"), v("ones", 0, 8), [[-16, 8]], A.is_equal, -1, 1)
+    iota(v("pcol"), [[0, 4]], 0, 1, False)
+    iota(v("ei"), [[2, 64]], 0, 128, False)
+    ts(v("pand"), v("pcol"), 4, A.logical_shift_right, 1, A.bitwise_and)
+    copy(v("mg1"), v("pand"))
+    ts(v("mg0"), v("pand"), -1.0, A.mult, 1.0, A.add)
+    ts(v("ei"), v("ei"), 2047, A.bitwise_and)
+    copy(v("ev"), v("ei"))
+    at("c3")
     for c in range(4):
-        if not PAR["s1"]:
-            tt(blk("a1", c), ind("x0s", "ln", 32 * c, 32 * c + 32), own_x(0, c // 2, 512 * (c % 2), 512, True), A.add)
-        dma("s", blk("a1c", c), blk("a1", c), "qc%d" % c, 128)
-    gains(0, "p1", False, PAR["par1"])
-    act(v("gout1"), v("gs", 0, 64))
+        iota(blk("kw", c), [[-1, 512]], 2047 - 512 * c, 0, True)
+        if S["zero"] == "g":
+            iota(blk("bc", c), [[0, 512]], 0, 0, True)
+        else:
+            mset(blk("bc", c), 0.0)
+    dma("s", v("bc", p=LROW), v("kw", p=LROW), 64)
+    at("c4")
+    for n in range(2):
+        mset(y(("tf%d" if S["je"] == "a" else "th%d") % n, 0, 9 * S["jq"] - 1), 0.0)
+
+    w1, w2 = (256 if "f" in S["par1"] else 128), (256 if "f" in S["par2"] else 128)
+    at("ln")
+    copy(v("ln", 0, 128), v("su32", 0, 128))
+    if f1 or f2:
+        copy(v("ln", 128, 256), v("su32", 128, 256))
+    exchange("ln", "p1", 0, "ap1", w1)
+    at("ln2")
+    exchange("ln", "p2", 1, "ap2", w2)
+    at("j0")
+    ts(v("lo"), v("su32", 0, 128), 15, A.bitwise_and)
+    copy(v("lob"), v("lo"))
+    dma("s", v("j0", p=JROW), v("lob"), 32)
+    tt(v("hib"), v("su32", 0, 128), v("lo"), A.subtract)
+    dma("s", v("j0", p=ROW), v("hib"), 32)
+    ps = bank()
+    mms([(v(ps, 0, 128), v("idm"), v("lob"), True, False), (v(ps, 0, 128), v("ids"), v("hib"), False, True)])
+    copy(v("lw"), v(ps, 0, 128))
+    at("sb")
+    copy(v("suh"), v("su32", 0, 128))
+    ps = bank()
+    mms([(v(ps, 16 * u, 16 * u + 16), v("idh"), v("suh", u, 128, 8), True, True) for u in range(8)])
+    ts(z("zb", 0), v(ps, 0, 128), v("mg0", 0, 1), A.mult)
+    ts(z("zb", 1), v(ps, 0, 128), v("mg1", 0, 1), A.mult)
+    turn(z("zo"), z("zb"))
+    tt(v("sb"), z("zo", 0), z("zo", 1), A.add)
+    tt(v("ds"), od("sb"), ev("sb"), A.subtract)
+    if S["ride"]:
+        dma("s", v("kw", p=JROW), v("sb"), 64)
+    at("nq")
+    tt(v("t3"), ev("lab32"), od("lab32"), A.not_equal)
+    ts(v("nq"), v("t3"), 2048.0, A.mult)
+    at("sb")
+    tt(v("d1"), v("ds"), v("t3"), A.mult)
+
+    beta1, beta2 = (16 * 129 - 7.5) / 8, (512 * 129 - 248) / 16
+    at("og1")
+    gather("og", "x0s", "ln", S["og1"])
+    at("par1")
+    if "g" in S["par1"]:
+        gather("oh", "x0s", "p1", S["pg1"], S["par1"])
+    gp = gains("x0s", "x0c", "p1", ("p1", 128), "oh", "mm", S["par1"], S["pr1"])
+    act(v("gout1"), gp, None, 4096.0)
     exchange("gout1", "gin1", 0, "ag1")
-    for hf in range(2):
-        kclear(hf); expand16("vph", hf, False)
-    gains(0, "ln", True, PAR["own1"], PAR["s1"])
-    tt(v("gh"), v("gin1"), v("ee"), A.add)
-    keyout(0)
-    jstep("ja", "j0", "lw", "e0"); copy(v("k1"), v("e0", 0, 128))
-    jstep("jb", "ja", "k1", "e1"); copy(v("k2"), v("e1", 0, 128))
-    jstep("ja", "jb", "k2", "e0"); copy(v("k3"), v("e0", 0, 128))
-    astep("ab", "a1", "a1c", "k1", True, -1)
-    astep("aa", "ab", "ac", "k2", True, 0)
-    astep("ab", "aa", "ac", "k3", False, 1)
-    for h in range(2):
-        act(blk("x1n", h, 1024), blk("ab", h, 1024), bias=255.5 - 1.0 / 32, scale=-1.0 / 16)
-        dma("s", blk("x1c", h, 1024), blk("x1n", h, 1024), "qx%d" % h, 256)
+    at("fs1")
+    first_sums("x0s", "og", S["fs1"], beta1, S["a12"])
+    at("own1")
+    gs = gains("x0s", "x0c", "ln", ("ln", 128), "og", "rr", S["own1"], S["or1"])
+    at("key1")
+    tt(v("t1"), gs, v("gin1"), A.add)
+    keys(0)
+    at("j1")
+    jstep("ja", "j0", "lw", "k1", S["j1"][0:2])
+    if S["ride"] < 2:
+        at("j2")
+        jstep("jb", "ja", "k1", "k2", S["j1"][2:4])
+    if S["ride"] < 1:
+        at("j3")
+        jstep("ja", "jb", "k2", "k3", S["j1"][4:6])
+    at("b11")
+    bstep("ba", "kw", "ln", "vvvv", ROW)
+    at("b12")
+    bstep("bb", "ba", "k1", "vvvv", ROW)
+    if S["ride"] >= 2:
+        at("j2")
+        jlist("bb", "k2")
+    at("b13")
+    bstep("ba", "bb", "k2", S["b14"], ROW)
+    if S["ride"] >= 1:
+        at("j3")
+        jlist("ba", "k3")
+    at("b14")
+    bstep("bb", "ba", "k3", "----", ROW, S["b14"])
+    bk = to_block("bb", 1, S["te"][0], "ba" if "a" in S["b14"] else None)[0]
+    sums("1", "x0s", "og", ["k1", "k2"], S["a12"], S["a13"], S["a14"], 0.0, 1, beta1)
+    at("a41")
+    astep("x1n", "aa", "k3", S["a14"], "----")
+    if f2:
+        for c in range(4):
+            dma("s", blk("x1c", c), blk("x1n", c), 128)
 
-    bstep("ba", "key", "lv", True, True)
-    bstep("bb", "ba", "k1", True)
-    bstep("ba", "bb", "k2", True)
-    bstep("bb", "ba", "k3", False)
-    for h in range(2): extract("e1", "bb", h, "wf")
-    gains(1, "p2", False, PAR["par2"])
-    act(v("gout2"), v("gs", 0, 64))
+    at("par2")
+    if "g" in S["par2"]:
+        gather("oh", "x1n", "p2", S["pg2"], S["par2"])
+    gp = gains("x1n", "x1c", "p2", ("p2", 128), "oh", "mm", S["par2"], S["pr2"])
+    act(v("gout2"), gp, None, 16 * 4096.0)
     exchange("gout2", "gin2", 1, "ag2")
-    for hf in range(2):
-        kclear(hf); expand16("vph", hf, False)
-    gains(1, "lq", True, PAR["own2"])
+    if not S["new2"]:
+        at("own2")
+        if "g" in S["own2"]:
+            gather("og", "x1n", "ln", S["og2"], S["own2"])
+        gs = gains("x1n", "x1c", "ln", ("ln", 128), "og", "rr", S["own2"], S["or2"])
 
-    def merges(m):
-        ts(v("wv"), v("bi"), 2047, A.bitwise_and)
-        tt(v("eq"), ev("bi"), od("bi"), A.is_equal)
-        tt(v("iq"), ev("wv"), v("vp1"), A.is_equal)
-        tt(v(m), v("iq"), v("eq"), A.mult)
-        copy(v("lt"), v("wv"))
-        tt(v("thb"), v("thi"), v(m), A.mult)
-        tt(v("tlb"), v("tlo"), v(m), A.mult)
+    at("m1")
+    bn = bk[1][0][0]
+    act(v("bo"), v(bn, 1, 128, 2))
+    tt(v("mn"), v(bn, 0, 128, 2), ev("key"), A.is_equal)
+    at("nq2")
+    tt(v("nq"), v(bn, 0, 128, 2), v("bo"), A.not_equal)
+    at("m1")
+    tt(v("m1"), v("mn"), v("nq"), A.is_gt)
+    swap("sn", "sb", "m1", "d1")
+    dma("s", v("kw", p=JROW), v("sn"), 64)
+    to_list(v("sn"), "n0")
+    at("on2")
+    gather("on", "x1n", "n0", S["on2"])
+    if S["new2"]:
+        at("own2")
+        gs = gains("x1n", "x1c", "n0", None, "on", "rr", "gggg", S["or2"])
+    at("key2")
+    tt(v("t0"), gs, v("gin2"), A.add)
+    lin(S["ko"][2], v("t1"), v("t0"), 0.0, 128.0)
+    keys(1)
 
-    ts(v("bi"), v("e1", 0, 128), 2048.0, A.mult)
-    merges("m1")
-    ts(v("ee"), v("eq"), -16384.0, A.mult)
-    tt(v("gh"), v("gin2"), v("ee"), A.add)
-    keyout(1)
-    swap("qf2", "qf", "dq", "m1", "md")
-    copy(v("lq2"), v("qf2"))
-    copy(v("si"), v("qf2"))
-    ts(v("lo"), v("si"), 15, A.bitwise_and)
-    jwindow("qf2", "lw2", "e0")
-    twindow()
+    at("fs2")
+    first_sums("x1n", "on", S["fs2"], beta2 - 2 * 2064.0, S["a22"])
+    for n, (o, w) in enumerate((("ba", "kw"), ("bb", "ba"), ("ba", "bb"), ("bb", "ba"))):
+        at("b2%d" % (n + 1))
+        bstep(o, w, "n%d" % n, S["b25"] if n == 3 else "vvvv", BL)
+        at("jl%d" % (n + 1))
+        jlist(o, "n%d" % (n + 1))
+    at("b25")
+    bstep("ba", "bb", "n4", "----", BL, S["b25"])
+    bk, lk = to_block("ba", 2, S["te"][1], "bb" if "a" in S["b25"] else None)
+    at("m2")
+    tt(v("ub"), bk, v("key"), A.subtract)
+    act(v("lb"), lk, None, 2047.0 / 4096, -1.0 / 4096)
+    tt(v("t1"), ev("ub"), od("ub"), A.add)
+    tt(v("mn"), ev("lb"), od("lb"), A.min)
+    tt(v("t2"), v("t1"), v("mn"), A.add)
+    tt(ev("tb"), ev("lb"), v("t2"), A.min)
+    tt(od("tb"), od("lb"), v("t2"), A.min)
+    dma("s", v("kw", p=ROW), v("tb"), 64)
+    at("lf")
+    copy(v("bi"), bk)
+    ts(v("wv"), v("bi"), 2047, A.bitwise_and)
+    to_list(v("wv"), "lf")
+    at("ysu")
+    ts(v("m1"), v("t1"), 0.0, A.is_equal)
+    swap("sf", "sn", "m1", "ds")
+    dma("s", hbm(T.ysu[:]), v("sf"), 64)
+    at("lab")
+    nl = len(S["lg"])
+    for h in range(nl):
+        w = 2048 // nl
+        lin(S["lg"][h], blk("bb", h, w), ind("kw", "lf", w // 16 * h, w // 16 * (h + 1)), 0.0, 4096.0)
+        dma("s", hbm(T.ylab[:, w * h:w * (h + 1)]), blk("bb", h, w, p=ROW), 64 // nl)
 
-    jstep("ja", "j0", "lw2", "e0"); copy(v("n1"), v("e0", 0, 128))
-    jstep("tg", "tw", "lt", "gs")
-    tt(v("t1"), v("gs", 0, 128), v("lc"), A.add)
-    ts(v("si"), v("t1"), -1.0, A.mult, 8192.0, A.add)
-    tt(v("l1"), v("si"), v("lc"), A.min)
-    ts(v("bq"), v("si"), 1, A.bitwise_and)
-    ts(v("vi"), v("si"), 1, A.logical_shift_right)
-    ts(v("t2"), v("bq"), 1024.0, A.mult)
-    tt(v("t3"), v("t2"), v("vi"), A.add)
-    ts(v("lm"), v("t3"), 2048.0, A.min)
-    tt(v("ts"), ev("l1"), od("l1"), A.min)
-    ts(v("ti"), v("ts"), -1.0, A.mult, 2048.0, A.add)
-    ts(v("thi"), v("ti"), 4080, A.bitwise_and); ts(v("tlo"), v("ti"), 15, A.bitwise_and)
-    jstep("jb", "ja", "n1", "e1"); copy(v("n2"), v("e1", 0, 128))
-    jstep("ja", "jb", "n2", "e0"); copy(v("n3"), v("e0", 0, 128))
-    jstep("jb", "ja", "n3", "e1"); copy(v("n4"), v("e1", 0, 128))
-    if PAR["s2"]:
-        first_sums(1, "aa", "lq2", False)
-    else:
-        astep("aa", "x1n", "x1c", "lq2", True, 2)
-    bstep("ba", "key", "lv", True, True)
-    bstep("bb", "ba", "k1", True)
-    bstep("ba", "bb", "k2", True)
-    bstep("bb", "ba", "k3", False)
-    for h in range(2): extract("d0", "bb", h, "wf")
-    act(v("t2"), v("d0", 0, 128))
-    for h in range(2):
-        act(blk("ba", h, 1024), ind("bb", "lm", 64 * h, 64 * h + 64))
-        extract("d1", "ba", h, "wf")
-    tt(v("t3"), v("d1", 0, 128), v("t2"), A.max)
-    ts(v("bi"), v("t3"), 2048.0, A.mult)
-    merges("m2")
-    twindow()
-    tt(v("iq"), v("m1"), v("m2"), A.add)
-    swap("sf", "sn", "ds", "iq", "md")
-    store("sf", "cm", "d0", "os1", T.ysu, "qy2", 0)
-    jstep("tg", "tw", "lt", "gs")
-    act(v("t1"), v("gs", 0, 128), bias=2048.0, scale=-1.0)
-    tt(v("lf"), v("t1"), v("l1"), A.min)
-    store("lf", "cn", "d1", "os2", T.ylab, "qy3", PAR["cn"])
-    astep("ab", "aa", "ac", "n1", True, 3)
-    astep("aa", "ab", "ac", "n2", True, 4)
-    astep("ab", "aa", "ac", "n3", True, 5)
-    w = 1024 // PAR["nq"]
-    for hf in range(PAR["nq"]):
-        for b in range(2):
-            c = 1024 * b + w * hf
-            tt(v("aa", c, c + w), ind("ab", "n4", c // 16, (c + w) // 16), v("ac", c, c + w), A.add)
-            act(v("yb", c, c + w), v("aa", c, c + w), bias=0.5 - 1.0 / 64, scale=1.0 / 32)
-            o = v("yo", 2 * w * hf + b, 2 * w * (hf + 1), 2)
-            if (2 * hf + b) * w < 512 * PAR["yo"]:
-                act(o, v("yb", c, c + w), bias=255.0, scale=-1.0)
-            else:
-                ts(o, v("yb", c, c + w), -1.0, A.mult, 255.0, A.add)
-        dma("s", hbm(T.yx[:, 2 * w * hf:2 * w * (hf + 1)]), blk("yo", hf, 2 * w), "qo%d" % hf, w // 2)
+    sums("2", "x1n", "on", ["n1", "n2"], S["a22"], S["a23"], S["a24"], 2064.0, 16, beta2)
+    at("a42")
+    astep("ab", "aa", "n3", S["a24"], S["a25"])
+    at("a52")
+    astep("yb", "ab", "n4", S["a25"], "----")
+    for c in range(4):
+        at("fin")
+        lin(S["fin"][c], blk("yo", c), blk("yb", c), -129.0, 1.0 / 512)
+        dma("s", hbm(T.yx[:, 512 * c:512 * (c + 1)]), blk("yo", c), 128)
+    return ops, nsent[0], len(use)
 
-    if "order" not in ORDER:
-        acc, deps = {}, []
-        for n, o in enumerate(ops):
-            dep = set(o[8])
-            for lst, isw in ((o[2], False), (o[3], True)):
-                for (name, lo, hi, p) in lst:
-                    for (m, l2, h2, p2, w2) in acc.get(name, []):
-                        if name in PS:
-                            if ops[m][0] != o[0] or w2 or isw:
-                                dep.add(m)
-                        elif (w2 or isw) and l2 < hi and lo < h2 and not (p and p2 and len(p) == len(p2) == 3 and p != p2):
+
+def depend(ops):
+    acc, deps = {}, []
+    for n, o in enumerate(ops):
+        dep = set(o[8])
+        for lst, isw in ((o[2], False), (o[3], True)):
+            for (name, lo, hi, p) in lst:
+                for (m, l2, h2, p2, w2) in acc.get(name, []):
+                    if name[0] == "#":
+                        if ops[m][0] != o[0] or w2 or isw:
                             dep.add(m)
-            deps.append(dep)
-            for lst, isw in ((o[2], False), (o[3], True)):
-                for (name, lo, hi, p) in lst:
-                    if name in PS and isw:
-                        acc[name] = []
-                    acc.setdefault(name, []).append((n, lo, hi, p, isw))
-        ORDER["order"], ORDER["deps"] = schedule(ops, deps), deps
-    order, deps = ORDER["order"], ORDER["deps"]
+                    elif (w2 or isw) and l2 < hi and lo < h2 and p & p2:
+                        dep.add(m)
+        dep.discard(n)
+        deps.append(dep)
+        for lst, isw in ((o[2], False), (o[3], True)):
+            for (name, lo, hi, p) in lst:
+                if name[0] == "#" and isw:
+                    acc[name] = []
+                elif isw:
+                    acc[name] = [x for x in acc.get(name, []) if not (lo <= x[1] and x[2] <= hi and x[3] & ~p == 0)]
+                acc.setdefault(name, []).append((n, lo, hi, p, isw))
+    return deps
+
+
+def rank_program(g, core, T, topo):
+    if T.rank_of(core) is None:
+        return
+    eng = {"v": g.vector, "a": g.scalar, "p": g.tensor, "g": g, "s": g.sync}
+    csem = {"v": "cv", "a": "ca", "p": "cp", "g": "cg"}
+    banks = {"#%d" % (n + 1): int(c) for n, c in enumerate(BK)}
+    ops, nsent, nuse = record(core, T, topo, banks)
+    order, deps = [int(k) for k in SEQ.split()], depend(ops)
+    holder, readers = {}, {}
+    for k in order:
+        for a in ops[k][3]:
+            if a[0] in banks and holder.get(banks[a[0]]) != a[0]:
+                deps[k].update(readers.get(holder.get(banks[a[0]]), []))
+                holder[banks[a[0]]] = a[0]
+        for a in ops[k][2]:
+            if a[0] in banks:
+                readers.setdefault(a[0], []).append(k)
     pos = {k: n for n, k in enumerate(order)}
     clock = {q: {} for q in eng}
     snap, waits, need = {}, {}, set()
@@ -511,9 +547,9 @@ def rank_program(g, core, T, topo):
         if o[5] == "c" and k in need:
             total[csem[o[0]]] = count[k] = total.get(csem[o[0]], 0) + 1
         elif o[5] == "d":
-            total[o[4]] = count[k] = total.get(o[4], 0) + 16
+            count[k] = 16
         elif o[5] == "x":
-            count[k] = len(use)
+            count[k] = nuse
     for k in order:
         q, fn, sem, kind = ops[k][0], ops[k][1], ops[k][4], ops[k][5]
         if kind == "x":
@@ -525,6 +561,7 @@ def rank_program(g, core, T, topo):
             ins.then_inc(T.sem[csem[q]], 1)
         elif kind == "d":
             ins.then_inc(T.sem[sem], 16)
-    g.wait_ge(T.sem.sent, nsent[0])
-    for s in ["qy2", "qy3"] + ["qo%d" % c for c in range(PAR["nq"])]:
-        g.wait_ge(T.sem[s], 16)
+    g.wait_ge(T.sem.sent, nsent)
+    for k in order:
+        if ops[k][5] == "d" and k not in need:
+            g.wait_ge(T.sem[ops[k][4]], 16)

@@ -3,30 +3,30 @@ from concourse.mybir import AluOpType, ActivationFunctionType
 F, B, H, I, U = "float32", "bfloat16", "float16", "int32", "uint16"
 SCRATCH = {}
 for _d, _w, _names in [
-    (B, 2048, "x0s x0c x1n x1c og oh on g2 g3 yb yo j0 ja jb"), (B, 4096, "rr mm"),
+    (B, 2048, "x0s x0c x1n x1c og oh on g2 g3 wa wb wc yb yo j0 ja jb"), (B, 4096, "rr mm"),
     (F, 2048, "aa ab ac ba bb bc kw gw"),
-    (B, 128, "idb idn idm ids hib lob"), (B, 144, "wd wdn"), (F, 128, "id32 ones key sb sn sf ub lb tb"), (H, 128, "idh suh"),
+    (B, 128, "idb idn idm ids hib lob"), (B, 144, "wd"), (F, 144, "tk"), (B, 8, "gmp gmn"),
+    (F, 64, "pps ppd"), (F, 128, "in1 ik0 ik1 id32 ones key sb sn sf lb tb"), (H, 128, "idh suh"),
     (F, 8, "gm1 gm selj"), (F, 16, "selb"), (I, 4, "pcol pand"), (F, 4, "mg1 mg0"),
     (I, 256, "su32"), (I, 128, "lo lab32 bi wv"), (F, 256, "tq tp2"),
     (U, 256, "ln p1 p2"), (U, 128, "lw k1 k2 k3 n0 n1 n2 n3 n4 lf"),
-    (F, 64, "ev ds md gout1 gout2 gin1 gin2 nq d1 t0 bo t1 t2 t3 m1 mn"), (I, 64, "ei"),
+    (F, 64, "ev ds md gout1 gout2 gin1 gin2 nq d1 t2 m1 mn"), (I, 64, "ei"),
 ]:
     for _n in _names.split():
         SCRATCH[_n] = ("sbuf", [128, _w], _d)
-for _n in ("tf0", "tf1", "th0", "th1"):
-    SCRATCH[_n + "2"] = ("sbuf", [128, 17, 8], F if _n[1] == "f" else H)
-    SCRATCH[_n + "4"] = ("sbuf", [128, 35, 4], F if _n[1] == "f" else H)
+for _n in ("tf0", "tf1"):
+    SCRATCH[_n] = ("sbuf", [128, 17, 8], F)
 for _n in ("zb", "zo"):
     SCRATCH[_n] = ("sbuf", [128, 8, 32], H)
 for _n in range(8):
     SCRATCH["ps%d" % _n] = ("psum", [128, 512], F)
-SEMAPHORES = "cv ca cp cg sent ap1 ap2 ag1 ag2".split() + ["q%d" % _c for _c in range(120)]
+SEMAPHORES = "cv ca cp cg sent ap1 ap2 ag1 ag2".split() + ["q%d" % _c for _c in range(100)]
 A = AluOpType
 AF = ActivationFunctionType
 PAR = dict(cy=0.85e-3, gather=1.56, pe=0.43e-3, fix=0.06, dma=1.9, bw=4.0e5, rem=3.0, first=2.0, hop=0.08)
-SPLIT = {'own1': 'gggg', 'par1': 'ffgg', 'own2': 'gggg', 'par2': 'gggg', 'og1': 'av', 'pg1': 'aa', 'og2': 'aa', 'on2': 'aa', 'pg2': 'aa', 'or1': 'vvaaaaaa', 'pr1': 'aaaaaaaa', 'or2': 'aaaaaaaa', 'pr2': 'aaaaaaaa', 'fs1': 'aaaa', 'fs2': 'aaaa', 'j1': 'vvaaaa', 'a12': 'vvvv', 'a13': 'vvvv', 'a22': 'aavv', 'a23': 'aavv', 'jq': 2, 'je': 'a', 'fin': 'aaaa', 'lg': 'av', 'zero': 'g', 'te': 'aa', 'new2': 0, 'ride': 0, 'b14': 'vvvv', 'b25': 'vaaa', 'a14': 'vvvv', 'a24': 'vvvv', 'a25': 'vvvv', 'ko': 'aaa'}
-SEQ = '31 2 38 1 0 39 3 8 5 6 9 7 10 20 16 23 15 19 4 17 22 30 18 24 40 53 41 54 46 25 42 43 26 47 63 49 48 64 51 50 92 55 56 95 93 27 60 11 28 98 52 12 96 94 57 21 131 115 34 13 99 89 97 119 90 35 100 121 134 116 132 91 122 33 113 65 133 135 71 29 136 185 120 107 76 32 140 74 189 186 80 36 82 66 190 81 101 58 44 45 141 37 83 183 68 75 103 142 184 59 137 109 70 187 14 138 67 114 188 77 139 69 61 193 146 72 73 78 79 197 194 84 85 108 102 147 198 86 195 105 143 87 88 191 196 104 110 192 144 148 106 145 202 111 112 117 118 200 123 124 125 126 127 199 128 130 129 201 62 204 149 203 219 151 150 223 217 155 152 207 224 153 156 232 205 225 154 157 211 213 212 159 158 240 208 163 236 160 206 161 214 234 164 209 210 233 215 162 165 216 167 166 218 246 171 168 226 248 220 252 169 172 241 242 170 173 247 221 222 227 237 228 174 177 229 235 230 231 254 176 249 178 255 175 238 239 253 244 179 243 180 245 181 182 250 258 251 259 260 256 261 257 262 263 273 264 274 265 267 266 275 268 276 269 277 279 270 278 272 271 284 292 287 290 293 288 280 296 298 291 289 294 297 282 299 285 300 295 302 281 301 286 308 283 306 303 309 392 304 305 314 307 395 310 312 396 311 315 316 398 397 313 393 317 318 399 400 394 322 401 319 402 320 321 323 324 403 326 325 330 404 328 327 405 331 406 410 332 329 334 333 411 338 407 335 340 339 336 408 355 337 412 343 409 341 413 356 344 357 342 345 418 347 346 419 414 352 358 351 415 348 349 350 360 416 353 361 420 417 354 362 421 424 359 363 366 430 364 367 422 365 369 431 368 426 371 370 376 427 372 383 373 377 374 378 375 379 423 380 428 425 381 429 384 432 382 385 388 386 433 390 387 389 391'
-BK = '1005602623463245157023777135552760431727346016213064572605326413726541031470'
+SPLIT = {'own1': 'gggg', 'par1': 'ffgg', 'own2': 'ggff', 'par2': 'gggg', 'og1': 'av', 'pg1': 'aa', 'og2': 'aa', 'on2': 'av', 'pg2': 'aa', 'or1': 'aaaaaaav', 'pr1': 'aaaaaaaa', 'or2': 'aaaaaaaa', 'pr2': 'aaaaaaaa', 'fs1': 'aaaa', 'fs2': 'aaaa', 'j1': 'vvaaaa', 'a12': 'vvvv', 'a13': 'vvvv', 'a22': 'aaav', 'a23': 'aaaa', 'fin': 'aaav', 'lg': 'aavv', 'te': 'aa', 'b14': 'vaaa', 'b25': 'aaaa', 'a14': 'vvvv', 'a24': 'vvvv', 'a25': 'vwvv', 'ko': 'aaa', 'go': 'aa'}
+SEQ = '29 0 6 1 2 7 28 3 4 10 5 11 9 8 22 27 23 24 26 15 19 42 18 30 13 44 16 52 17 33 14 46 12 47 41 53 55 54 31 57 56 68 32 45 58 48 49 69 20 90 21 93 129 91 96 92 107 97 35 99 94 132 98 130 100 39 95 108 101 131 133 37 66 135 182 40 134 112 183 75 70 136 71 50 51 38 137 102 184 138 82 77 188 36 185 79 186 189 84 78 114 83 72 187 139 80 73 74 43 85 119 141 76 190 81 86 104 140 191 192 117 87 113 88 89 196 142 193 103 109 194 197 115 105 143 195 25 120 118 106 198 110 144 111 199 202 116 121 122 203 59 123 34 60 124 145 125 61 126 62 127 63 128 146 64 200 201 204 147 205 207 149 148 206 151 223 150 220 153 152 218 215 224 154 155 221 213 157 208 231 156 210 159 158 225 211 161 234 160 209 239 65 162 163 219 232 212 214 237 165 164 216 172 166 226 217 222 240 227 167 173 228 235 229 230 248 67 174 168 169 175 246 170 177 178 242 171 179 245 176 180 233 238 181 236 243 249 251 250 241 253 244 252 254 247 255 264 256 257 265 258 266 259 267 260 268 269 261 270 263 262 277 282 273 278 271 274 280 283 279 275 272 286 288 281 276 284 287 289 290 291 292 285 298 388 296 293 389 299 385 294 295 304 297 390 302 391 386 394 303 305 392 387 300 306 393 307 308 301 312 395 314 396 313 309 399 310 311 320 315 318 403 400 316 321 319 397 322 404 407 317 323 398 328 324 405 329 408 406 325 401 326 332 409 327 402 331 410 344 333 330 334 345 335 411 341 336 414 412 346 337 340 338 415 347 339 416 342 349 350 413 417 343 351 355 348 418 352 419 354 353 424 358 422 356 359 365 425 357 420 360 361 366 363 362 367 364 373 369 368 375 421 370 423 371 428 372 426 429 374 430 376 377 383 427 431 379 381 384 378 380 382'
+BK = '075542612350344507623671114043370562142716253014657321763270437045316270540516524'
 
 
 def record(core, T, topo, banks):
@@ -46,7 +46,8 @@ def record(core, T, topo, banks):
         b = w if b is None else b
         ps = slice(None) if p is None else slice(p[0], p[1], p[2] if len(p) > 2 else None)
         pm = ALL if p is None else sum(1 << x for x in range(128)[ps])
-        return (T[real][ps, a:b:s] if s else T[real][ps, a:b], [(name, a, b, pm)], len(range(a, b, s or 1)), size[SCRATCH[real][2]], name[0] == "#")
+        return (T[real][ps, a:b:s] if s else T[real][ps, a:b], [(name, a, b, pm, a % 2 if s == 2 else None)], len(range(a, b, s or 1)),
+                size[SCRATCH[real][2]], name[0] == "#")
 
     def blk(name, c, n=512, p=None): return v(name, n * c, n * c + n, p=p)
     def ev(n): return v(n, 0, 128, 2)
@@ -59,9 +60,7 @@ def record(core, T, topo, banks):
             return (T[name][:, :, 16 * half:16 * half + 16], [(name, 16 * half, 16 * half + 16, ALL)], 128, 2, False)
         return (T[name][:, u, 16 * half:16 * half + 16], [(name, 16 * half, 16 * half + 16, ALL)], 16, 2, False)
 
-    def y(name, a, b, s=1):
-        name += str(S["jq"])
-        return (T[name][:, a:b:s, :], [(name, 0, 35, ALL)], 16 // S["jq"] * len(range(a, b, s)), size[SCRATCH[name][2]], False)
+    def y(name, a, b, s=1): return (T[name][:, a:b:s, :], [(name, 0, 17, ALL)], 8 * len(range(a, b, s)), 4, False)
 
     def ind(win, lst, c, d):
         return (T[win][:, 0:SCRATCH[win][1][1]].indirect(T[lst][:, c:d]), [(win, 0, 1 << 20, ALL), (lst, c, d, ALL)], 16 * (d - c), 4, "ind")
@@ -108,9 +107,6 @@ def record(core, T, topo, banks):
         else:
             ts(o, i, 0.0, A.max)
 
-    def mm(o, l, r, st, sp):
-        rec("p", lambda e: e.matmul(o[0], l[0], r[0], st, sp), [l, r], [o], max(min(64, l[2]), r[2]) * l[3] * l[3] / 4 * PAR["pe"])
-
     def mms(calls):
         def fn(e):
             for (o, l, r, st, sp) in calls:
@@ -118,6 +114,8 @@ def record(core, T, topo, banks):
             return ins
         rec("p", fn, sum([[c[1], c[2]] for c in calls], []), [c[0] for c in calls],
             sum(max(min(64, l[2]), r[2]) * l[3] * l[3] / 4 * PAR["pe"] for (o, l, r, st, sp) in calls))
+
+    def mm(o, l, r, st, sp): mms([(o, l, r, st, sp)])
 
     def aff(o, i, pat, cmp, base, cm): rec("g", lambda e: e.affine_select(o[0], i[0], pat, cmp, 0.0, base, cm), [i], [o], 0.17 + 2 * o[2] * cy)
 
@@ -171,26 +169,20 @@ def record(core, T, topo, banks):
     def to_block(src, n, q, prev=None):
         if prev:
             act(v("tq", 0, 128 * n), v(turned(prev, n), 0, 128 * n))
-        ps, out = turned(src, n), []
+        ps = turned(src, n)
         for r in range(n):
-            out.append(bank())
             if prev:
                 tt(blk("tp2", r, 128), blk(ps, r, 128), blk("tq", r, 128), A.max)
             else:
                 lin(q, blk("tp2", r, 128), blk(ps, r, 128))
-            mm(v(out[r], 0, 128), blk("tp2", r, 128), v("id32"), True, True)
-        return [v(o, 0, 128) for o in out]
 
     def jlist(src, dst):
-        n = S["jq"]
-        m, r = 128 // n, 16 // n
-        for c in range(n):
-            ps, p2 = bank(), bank()
-            tp, idm = ("tf%d" % (c % 2), "id32") if S["je"] == "a" else ("th%d" % (c % 2), "idh")
-            mms([(v(ps, i, 8 * r, r), v(src, 16 * m * c + i, 16 * m * (c + 1), r), v("selj"), True, True) for i in range(r)])
-            lin(S["je"], y(tp, n - 1, 9 * n - 1, n), v(ps, 0, 8 * r))
-            mms([(v(p2, 0, m), y(tp, n - 1 - b, 9 * n - 1 - b), v(idm, b, 128, n), b == 0, b == n - 1) for b in range(n)])
-            copy(v(dst, m * c, m * (c + 1)), v(p2, 0, m))
+        for c in range(2):
+            ps, p2, tp = bank(), bank(), "tf%d" % c
+            mms([(v(ps, i, 64, 8), v(src, 1024 * c + i, 1024 * (c + 1), 8), v("selj"), True, True) for i in range(8)])
+            act(y(tp, 1, 17, 2), v(ps, 0, 64))
+            mms([(v(p2, 0, 64), y(tp, 1 - b, 17 - b), v("id32", b, 128, 2), b == 0, b == 1) for b in range(2)])
+            copy(blk(dst, c, 64), v(p2, 0, 64))
 
     def jstep(out, win, lst, dst, who):
         for h in range(2):
@@ -208,18 +200,18 @@ def record(core, T, topo, banks):
             if keep[c] == "v":
                 dma("s", blk("bc", c, p=rows), blk(out, c, p=rows), 16 * 16 // rows[2])
 
-    def first_sums(x, og, who, bias, nxt):
+    def first_sums(x, og, who, bias, nxt, out="aa", cp="ac", kb=256):
         for c in range(4):
             d = bank()
             mms([(v(d), v("idb"), blk(x, c), True, False), (v(d), v("idb"), blk(og, c), False, True)])
-            lin(who[c], blk("aa", c), v(d), bias)
+            lin(who[c], blk(out, c), v(d), bias)
             if nxt[c] == "v":
-                dma("s", blk("ac", c), blk("aa", c), 256)
+                dma("s", blk(cp, c), blk(out, c), kb)
 
-    def astep(out, win, lst, who, nxt, parts=(), gbias=0.0, bias=0.0):
+    def astep(out, win, lst, who, nxt, parts=(), gbias=0.0, bias=0.0, cp="ac"):
         for c in range(4):
             if who[c] == "v":
-                tt(blk(out, c), ind(win, lst, 32 * c, 32 * c + 32), blk("ac", c), A.add)
+                tt(blk(out, c), ind(win, lst, 32 * c, 32 * c + 32), blk(cp, c), A.add)
             elif who[c] == "w":
                 act(blk("gw", c), ind(win, lst, 32 * c, 32 * c + 32))
                 d = bank()
@@ -233,12 +225,6 @@ def record(core, T, topo, banks):
             if nxt[c] == "v":
                 dma("s", blk("ac", c), blk(out, c), 256)
 
-    def sums(r, x, og, lists, s2, s3, s4, off, unit, beta):
-        at("a2" + r)
-        astep("ab", "aa", lists[0], s2, s3, [x, og, "g2"], -beta, 2 * beta - 2 * off)
-        at("a3" + r)
-        astep("aa", "ab", lists[1], s3, s4, [x, og, "g2", "g3"], -2 * beta - 256 * unit, 4 * beta - 2 * off + 256 * unit)
-
     def gather(og, x, lst, who, kind="gggg"):
         for h in range(2):
             a = 2 * h + (kind[2 * h] != "g")
@@ -246,12 +232,12 @@ def record(core, T, topo, banks):
             if a < b:
                 lin(who[h], v(og, 512 * a, 512 * b), ind(x, lst, 32 * a, 32 * b))
 
-    def gains(x, xc, lst, lsw, og, rr, kind, who):
+    def gains(x, xc, lst, og, rr, kind, who):
         ps = bank()
         for c in range(4):
             if kind[c] == "f":
                 tt(blk(rr, c), ind(x, lst, 32 * c, 32 * c + 32), blk(xc, c), A.max)
-                tt(blk(rr, 4 + c), ind(x, lsw[0], lsw[1] + 32 * c, lsw[1] + 32 * c + 32), blk(xc, c), A.max)
+                tt(blk(rr, 4 + c), ind(x, lst, 128 + 32 * c, 128 + 32 * c + 32), blk(xc, c), A.max)
             else:
                 d = bank()
                 mms([(v(d), v("idb"), blk(x, c), True, False), (v(d), v("idn"), blk(og, c), False, True)])
@@ -261,13 +247,18 @@ def record(core, T, topo, banks):
                      (v(d, 0, 512, 2), v("idn"), v(og, 512 * c + 1, 512 * c + 512, 2), False, False),
                      (v(d, 1, 512, 2), v("idn"), v(og, 512 * c, 512 * c + 512, 2), False, True)])
                 relu(who[2 * c + 1], blk(rr, 4 + c), v(d))
-            for t, mask in ((0, "wd"), (1, "wdn")):
-                mms([(v(ps, 0, 64), v(mask, 15 - k, 143 - k), v(rr, 2048 * t + 128 * k + b, 2048 * t + 128 * k + 128, 2),
-                      (c, t, k, b) == (0, 0, 0, 0), (c, t, k, b) == (3, 1, 15, 1)) for k in range(4 * c, 4 * c + 4) for b in range(2)])
+            mms([(v(ps, j, 64, 8), v(rr, 2048 * t + 256 * j + b, 2048 * t + 256 * j + 256, 2), v(("gmp", "gmn")[t]), t + b == 0, t + b == 2)
+                 for j in range(2 * c, 2 * c + 2) for t in range(2) for b in range(2)])
         return v(ps, 0, 64)
 
-    def keys(side):
-        tt(v("t2"), v("t1"), v("nq"), A.mult)
+    def halves(own, gin, side):
+        tt(v("tk", 1, 129, 2), own, v(gin), A.add)
+        ps = bank()
+        mms([(v(ps, 0, 64), v("tk", 1 - b, 129 - b), v("ik%d" % side, 64 * b, 64 * b + 64), b == 0, b == 1) for b in range(2)])
+        return v(ps, 0, 64)
+
+    def keys(h, side):
+        tt(v("t2"), h, v("nq"), A.mult)
         tt(ev("key"), v("t2"), v("ev"), A.add)
         lin(S["ko"][side], od("key"), ev("key"), float(side))
         dma("s", v("kw", p=ROW), v("key"), 64)
@@ -278,29 +269,31 @@ def record(core, T, topo, banks):
         tt(ev(out), ev(src), v("md"), A.add)
         tt(od(out), od(src), v("md"), A.subtract)
 
-    f1, f2 = "f" in S["par1"] + S["own1"], "f" in S["par2"] + S["own2"]
     at("ld")
     dma("s", v("su32", 0, 128), hbm(T.su[:]), 64)
     dma("a", v("x0s"), hbm(T.x0[:]), 512)
     at("ld2")
-    if f1 or f2:
-        dma("s", v("su32", 128, 256, p=(0, 128, 2)), hbm(T.su[1:128:2, :]), 32)
-        dma("s", v("su32", 128, 256, p=(1, 128, 2)), hbm(T.su[0:128:2, :]), 32)
+    dma("s", v("su32", 128, 256, p=(0, 128, 2)), hbm(T.su[1:128:2, :]), 32)
+    dma("s", v("su32", 128, 256, p=(1, 128, 2)), hbm(T.su[0:128:2, :]), 32)
     at("ld3")
     dma("s", v("lab32"), hbm(T.lab[:]), 64)
-    if f1:
-        dma("s", v("x0c"), hbm(T.x0[:]), 512)
+    dma("s", v("x0c"), hbm(T.x0[:]), 512)
     at("c1")
     mset(v("ones"), 1.0); mset(v("j0"), 0.0)
-    for n in ("wd", "wdn"):
-        mset(v(n), 0.0)
+    mset(v("wd"), 0.0)
     aff(v("id32"), v("ones"), [[-1, 128]], A.is_equal, 0, 1)
     aff(v("gm1"), v("ones", 0, 8), [[-16, 8]], A.is_ge, 0, 1)
     aff(v("gm"), v("gm1"), [[16, 8]], A.is_ge, 15, -1)
-    act(v("wd", 15, 143, 16), v("gm")); act(v("wdn", 15, 143, 16), v("gm"), scale=-1.0)
+    act(v("wd", 15, 143, 16), v("gm")); act(v("gmp"), v("gm")); act(v("gmn"), v("gm"), scale=-1.0)
     act(v("idb"), v("id32")); act(v("idn"), v("id32"), scale=-1.0)
     act(v("idm"), v("id32"), scale=128.0); act(v("ids"), v("id32"), scale=1.0 / 16)
     copy(v("idh"), v("id32"))
+    at("c5")
+    act(v("ik0"), v("id32"), scale=2048.0); act(v("ik1"), v("id32"), scale=128.0)
+    mset(v("tk"), 0.0)
+    act(v("in1"), v("id32"), scale=-1.0)
+    tt(v("pps"), ev("id32"), od("id32"), A.add)
+    tt(v("ppd"), ev("id32"), od("id32"), A.subtract)
     at("c2")
     aff(v("selb"), v("ones", 0, 16), [[-8, 2], [-16, 8]], A.is_equal, 0, 1)
     aff(v("selj"), v("ones", 0, 8), [[-16, 8]], A.is_equal, -1, 1)
@@ -314,23 +307,18 @@ def record(core, T, topo, banks):
     at("c3")
     for c in range(4):
         iota(blk("kw", c), [[-1, 512]], 2047 - 512 * c, 0, True)
-        if S["zero"] == "g":
-            iota(blk("bc", c), [[0, 512]], 0, 0, True)
-        else:
-            mset(blk("bc", c), 0.0)
+        iota(blk("bc", c), [[0, 512]], 0, 0, True)
     dma("s", v("bc", p=LROW), v("kw", p=LROW), 64)
     at("c4")
     for n in range(2):
-        mset(y(("tf%d" if S["je"] == "a" else "th%d") % n, 0, 9 * S["jq"] - 1), 0.0)
+        mset(y("tf%d" % n, 0, 17), 0.0)
 
-    w1, w2 = (256 if "f" in S["par1"] else 128), (256 if "f" in S["par2"] else 128)
     at("ln")
     copy(v("ln", 0, 128), v("su32", 0, 128))
-    if f1 or f2:
-        copy(v("ln", 128, 256), v("su32", 128, 256))
-    exchange("ln", "p1", 0, "ap1", w1)
+    copy(v("ln", 128, 256), v("su32", 128, 256))
+    exchange("ln", "p1", 0, "ap1", 256 if "f" in S["par1"] else 128)
     at("ln2")
-    exchange("ln", "p2", 1, "ap2", w2)
+    exchange("ln", "p2", 1, "ap2", 256 if "f" in S["par2"] else 128)
     at("j0")
     ts(v("lo"), v("su32", 0, 128), 15, A.bitwise_and)
     copy(v("lob"), v("lo"))
@@ -349,95 +337,77 @@ def record(core, T, topo, banks):
     turn(z("zo"), z("zb"))
     tt(v("sb"), z("zo", 0), z("zo", 1), A.add)
     tt(v("ds"), od("sb"), ev("sb"), A.subtract)
-    if S["ride"]:
-        dma("s", v("kw", p=JROW), v("sb"), 64)
     at("nq")
-    tt(v("t3"), ev("lab32"), od("lab32"), A.not_equal)
-    ts(v("nq"), v("t3"), 2048.0, A.mult)
+    tt(v("nq"), ev("lab32"), od("lab32"), A.not_equal)
     at("sb")
-    tt(v("d1"), v("ds"), v("t3"), A.mult)
+    tt(v("d1"), v("ds"), v("nq"), A.mult)
 
     beta1, beta2 = (16 * 129 - 7.5) / 8, (512 * 129 - 248) / 16
     at("og1")
     gather("og", "x0s", "ln", S["og1"])
     at("par1")
-    if "g" in S["par1"]:
-        gather("oh", "x0s", "p1", S["pg1"], S["par1"])
-    gp = gains("x0s", "x0c", "p1", ("p1", 128), "oh", "mm", S["par1"], S["pr1"])
-    act(v("gout1"), gp, None, 4096.0)
+    gather("oh", "x0s", "p1", S["pg1"], S["par1"])
+    gp = gains("x0s", "x0c", "p1", "oh", "mm", S["par1"], S["pr1"])
+    lin(S["go"][0], v("gout1"), gp, 4096.0)
     exchange("gout1", "gin1", 0, "ag1")
     at("fs1")
     first_sums("x0s", "og", S["fs1"], beta1, S["a12"])
     at("own1")
-    gs = gains("x0s", "x0c", "ln", ("ln", 128), "og", "rr", S["own1"], S["or1"])
+    gs = gains("x0s", "x0c", "ln", "og", "rr", S["own1"], S["or1"])
     at("key1")
-    tt(v("t1"), gs, v("gin1"), A.add)
-    keys(0)
+    keys(halves(gs, "gin1", 0), 0)
     at("j1")
     jstep("ja", "j0", "lw", "k1", S["j1"][0:2])
-    if S["ride"] < 2:
-        at("j2")
-        jstep("jb", "ja", "k1", "k2", S["j1"][2:4])
-    if S["ride"] < 1:
-        at("j3")
-        jstep("ja", "jb", "k2", "k3", S["j1"][4:6])
+    at("j2")
+    jstep("jb", "ja", "k1", "k2", S["j1"][2:4])
+    at("j3")
+    jstep("ja", "jb", "k2", "k3", S["j1"][4:6])
     at("b11")
     bstep("ba", "kw", "ln", "vvvv", ROW)
     at("b12")
     bstep("bb", "ba", "k1", "vvvv", ROW)
-    if S["ride"] >= 2:
-        at("j2")
-        jlist("bb", "k2")
     at("b13")
     bstep("ba", "bb", "k2", S["b14"], ROW)
-    if S["ride"] >= 1:
-        at("j3")
-        jlist("ba", "k3")
     at("b14")
     bstep("bb", "ba", "k3", "----", ROW, S["b14"])
-    bk = to_block("bb", 1, S["te"][0], "ba" if "a" in S["b14"] else None)[0]
-    sums("1", "x0s", "og", ["k1", "k2"], S["a12"], S["a13"], S["a14"], 0.0, 1, beta1)
+    to_block("bb", 1, S["te"][0], "ba" if "a" in S["b14"] else None)
+    at("a21")
+    astep("ab", "aa", "k1", S["a12"], S["a13"], ["x0s", "og", "g2"], -beta1, 2 * beta1)
+    at("a31")
+    astep("aa", "ab", "k2", S["a13"], S["a14"], ["x0s", "og", "g2", "g3"], -2 * beta1 - 256, 4 * beta1 + 256)
     at("a41")
     astep("x1n", "aa", "k3", S["a14"], "----")
-    if f2:
-        for c in range(4):
-            dma("s", blk("x1c", c), blk("x1n", c), 128)
+    for c in range(4):
+        dma("s", blk("x1c", c), blk("x1n", c), 128)
 
     at("par2")
-    if "g" in S["par2"]:
-        gather("oh", "x1n", "p2", S["pg2"], S["par2"])
-    gp = gains("x1n", "x1c", "p2", ("p2", 128), "oh", "mm", S["par2"], S["pr2"])
-    act(v("gout2"), gp, None, 16 * 4096.0)
+    gather("oh", "x1n", "p2", S["pg2"], S["par2"])
+    gp = gains("x1n", "x1c", "p2", "oh", "mm", S["par2"], S["pr2"])
+    lin(S["go"][1], v("gout2"), gp, 16 * 4096.0)
     exchange("gout2", "gin2", 1, "ag2")
-    if not S["new2"]:
-        at("own2")
-        if "g" in S["own2"]:
-            gather("og", "x1n", "ln", S["og2"], S["own2"])
-        gs = gains("x1n", "x1c", "ln", ("ln", 128), "og", "rr", S["own2"], S["or2"])
+    at("own2")
+    gather("og", "x1n", "ln", S["og2"], S["own2"])
+    gs = gains("x1n", "x1c", "ln", "og", "rr", S["own2"], S["or2"])
 
     at("m1")
-    bn = bk[1][0][0]
-    act(v("bo"), v(bn, 1, 128, 2))
-    tt(v("mn"), v(bn, 0, 128, 2), ev("key"), A.is_equal)
+    pt, pd = bank(), bank()
+    mms([(v(pt, 0, 64), v("in1"), ev("key"), True, False), (v(pt, 0, 64), v("in1"), od("key"), False, False)])
+    mm(v(pt, 0, 64), blk("tp2", 0, 128), v("pps"), False, True)
+    act(v("m1"), v(pt, 0, 64), AF.Relu, 1.0, -1.0)
     at("nq2")
-    tt(v("nq"), v(bn, 0, 128, 2), v("bo"), A.not_equal)
+    mm(v(pd, 0, 64), blk("tp2", 0, 128), v("ppd"), True, True)
+    ts(v("nq"), v(pd, 0, 64), 0.0, A.not_equal)
     at("m1")
-    tt(v("m1"), v("mn"), v("nq"), A.is_gt)
     swap("sn", "sb", "m1", "d1")
     dma("s", v("kw", p=JROW), v("sn"), 64)
     to_list(v("sn"), "n0")
     at("on2")
     gather("on", "x1n", "n0", S["on2"])
-    if S["new2"]:
-        at("own2")
-        gs = gains("x1n", "x1c", "n0", None, "on", "rr", "gggg", S["or2"])
     at("key2")
-    tt(v("t0"), gs, v("gin2"), A.add)
-    lin(S["ko"][2], v("t1"), v("t0"), 0.0, 128.0)
-    keys(1)
+    keys(halves(gs, "gin2", 1), 1)
 
     at("fs2")
-    first_sums("x1n", "on", S["fs2"], beta2 - 2 * 2064.0, S["a22"])
+    first_sums("x1n", "on", S["fs2"], -2 * 2064.0 - 16 * 127, S["a22"], "wa", "wc", 128)
     for n, (o, w) in enumerate((("ba", "kw"), ("bb", "ba"), ("ba", "bb"), ("bb", "ba"))):
         at("b2%d" % (n + 1))
         bstep(o, w, "n%d" % n, S["b25"] if n == 3 else "vvvv", BL)
@@ -445,32 +415,39 @@ def record(core, T, topo, banks):
         jlist(o, "n%d" % (n + 1))
     at("b25")
     bstep("ba", "bb", "n4", "----", BL, S["b25"])
-    bk, lk = to_block("ba", 2, S["te"][1], "bb" if "a" in S["b25"] else None)
+    to_block("ba", 2, S["te"][1], "bb" if "a" in S["b25"] else None)
     at("m2")
-    tt(v("ub"), bk, v("key"), A.subtract)
-    act(v("lb"), lk, None, 2047.0 / 4096, -1.0 / 4096)
-    tt(v("t1"), ev("ub"), od("ub"), A.add)
-    tt(v("mn"), ev("lb"), od("lb"), A.min)
-    tt(v("t2"), v("t1"), v("mn"), A.add)
-    tt(ev("tb"), ev("lb"), v("t2"), A.min)
-    tt(od("tb"), od("lb"), v("t2"), A.min)
+    pt, pl, pb = bank(), bank(), bank()
+    mm(v(pt, 0, 64), v("in1"), ev("key"), True, False)
+    mms([(v(pt, 0, 64), blk("tp2", 0, 128), ev("id32"), False, False), (v(pt, 0, 64), v("in1"), od("key"), False, False),
+         (v(pt, 0, 64), blk("tp2", 0, 128), od("id32"), False, True)])
+    act(v("m1"), v(pt, 0, 64), AF.Relu, 1.0, -1.0)
+    mm(v(pl, 0, 128), blk("tp2", 1, 128), v("id32"), True, True)
+    lin(S["ko"][2], v("lb"), v(pl, 0, 128))
+    tt(v("mn"), ev("lb"), od("lb"), A.max)
+    tt(v("t2"), v("mn"), v("m1"), A.mult)
+    tt(ev("tb"), ev("lb"), v("t2"), A.max)
+    tt(od("tb"), od("lb"), v("t2"), A.max)
     dma("s", v("kw", p=ROW), v("tb"), 64)
     at("lf")
-    copy(v("bi"), bk)
+    mm(v(pb, 0, 128), blk("tp2", 0, 128), v("id32"), True, True)
+    copy(v("bi"), v(pb, 0, 128))
     ts(v("wv"), v("bi"), 2047, A.bitwise_and)
     to_list(v("wv"), "lf")
     at("ysu")
-    ts(v("m1"), v("t1"), 0.0, A.is_equal)
     swap("sf", "sn", "m1", "ds")
     dma("s", hbm(T.ysu[:]), v("sf"), 64)
     at("lab")
     nl = len(S["lg"])
     for h in range(nl):
         w = 2048 // nl
-        lin(S["lg"][h], blk("bb", h, w), ind("kw", "lf", w // 16 * h, w // 16 * (h + 1)), 0.0, 4096.0)
+        lin(S["lg"][h], blk("bb", h, w), ind("kw", "lf", w // 16 * h, w // 16 * (h + 1)), 2047.0, -1.0)
         dma("s", hbm(T.ylab[:, w * h:w * (h + 1)]), blk("bb", h, w, p=ROW), 64 // nl)
 
-    sums("2", "x1n", "on", ["n1", "n2"], S["a22"], S["a23"], S["a24"], 2064.0, 16, beta2)
+    at("a22")
+    astep("wb", "wa", "n1", S["a22"], "----", ["wa", "g2"], cp="wc")
+    at("a32")
+    astep("aa", "wb", "n2", S["a23"], S["a24"], ["wb", "g3"], 0.0, 16 * 508 + 4 * beta2)
     at("a42")
     astep("ab", "aa", "n3", S["a24"], S["a25"])
     at("a52")
@@ -487,22 +464,22 @@ def depend(ops):
     for n, o in enumerate(ops):
         dep = set(o[8])
         for lst, isw in ((o[2], False), (o[3], True)):
-            for (name, lo, hi, p) in lst:
-                for (m, l2, h2, p2, w2) in acc.get(name, []):
+            for (name, lo, hi, p, *odd) in lst:
+                for (m, l2, h2, p2, w2, odd2) in acc.get(name, []):
                     if name[0] == "#":
                         if ops[m][0] != o[0] or w2 or isw:
                             dep.add(m)
-                    elif (w2 or isw) and l2 < hi and lo < h2 and p & p2:
+                    elif (w2 or isw) and l2 < hi and lo < h2 and p & p2 and {*odd, *odd2} != {0, 1}:
                         dep.add(m)
         dep.discard(n)
         deps.append(dep)
         for lst, isw in ((o[2], False), (o[3], True)):
-            for (name, lo, hi, p) in lst:
+            for (name, lo, hi, p, *odd) in lst:
                 if name[0] == "#" and isw:
                     acc[name] = []
-                elif isw:
+                elif isw and odd in ([], [None]):
                     acc[name] = [x for x in acc.get(name, []) if not (lo <= x[1] and x[2] <= hi and x[3] & ~p == 0)]
-                acc.setdefault(name, []).append((n, lo, hi, p, isw))
+                acc.setdefault(name, []).append((n, lo, hi, p, isw, odd))
     return deps
 
 

from concourse.mybir import AluOpType, ActivationFunctionType

F, B, H, I, U = "float32", "bfloat16", "float16", "int32", "uint16"
SCRATCH = {}
for _d, _w, _names in [
    (B, 2048, "x0s x0c x1n x1c og oh on g2 g3 wa wb wc yb yo j0 ja jb"), (B, 4096, "rr mm"),
    (F, 2048, "aa ab ac ba bb bc kw gw"),
    (B, 128, "idb idn idm ids hib lob"), (B, 144, "wd"), (F, 144, "tk"), (B, 8, "gmp gmn"),
    (F, 64, "pps ppd"), (F, 128, "in1 ik0 ik1 id32 ones key sb sn sf lb tb"), (H, 128, "idh suh"),
    (F, 8, "gm1 gm selj"), (F, 16, "selb"), (I, 4, "pcol pand"), (F, 4, "mg1 mg0"),
    (I, 256, "su32"), (I, 128, "lo lab32 bi wv"), (F, 256, "tq tp2"),
    (U, 256, "ln p1 p2"), (U, 128, "lw k1 k2 k3 n0 n1 n2 n3 n4 lf"),
    (F, 64, "ev ds md gout1 gout2 gin1 gin2 nq d1 t2 m1 mn"), (I, 64, "ei"),
]:
    for _n in _names.split():
        SCRATCH[_n] = ("sbuf", [128, _w], _d)
for _n in ("tf0", "tf1"):
    SCRATCH[_n] = ("sbuf", [128, 17, 8], F)
for _n in ("zb", "zo"):
    SCRATCH[_n] = ("sbuf", [128, 8, 32], H)
for _n in range(8):
    SCRATCH["ps%d" % _n] = ("psum", [128, 512], F)
SEMAPHORES = "cv ca cp cg sent ap1 ap2 ag1 ag2".split() + ["q%d" % _c for _c in range(100)]
A = AluOpType
AF = ActivationFunctionType
PAR = dict(cy=0.85e-3, gather=1.56, pe=0.43e-3, fix=0.06, dma=1.9, bw=4.0e5, rem=3.0, first=2.0, hop=0.08)
SPLIT = {'own1': 'gggg', 'par1': 'ffgg', 'own2': 'ggff', 'par2': 'gggg', 'og1': 'av', 'pg1': 'aa', 'og2': 'aa', 'on2': 'av', 'pg2': 'aa', 'or1': 'aaaaaaav', 'pr1': 'aaaaaaaa', 'or2': 'aaaaaaaa', 'pr2': 'aaaaaaaa', 'fs1': 'aaaa', 'fs2': 'aaaa', 'j1': 'vvaaaa', 'a12': 'vvvv', 'a13': 'vvvv', 'a22': 'aaav', 'a23': 'aaaa', 'fin': 'aaav', 'lg': 'aavv', 'te': 'aa', 'b14': 'vaaa', 'b25': 'aaaa', 'a14': 'vvvv', 'a24': 'vvvv', 'a25': 'vwvv', 'ko': 'aaa', 'go': 'aa'}
SEQ = '29 0 6 1 2 7 28 3 4 10 5 11 9 8 22 27 23 24 26 15 19 42 18 30 13 44 16 52 17 33 14 46 12 47 41 53 55 54 31 57 56 68 32 45 58 48 49 69 20 90 21 93 129 91 96 92 107 97 35 99 94 132 98 130 100 39 95 108 101 131 133 37 66 135 182 40 134 112 183 75 70 136 71 50 51 38 137 102 184 138 82 77 188 36 185 79 186 189 84 78 114 83 72 187 139 80 73 74 43 85 119 141 76 190 81 86 104 140 191 192 117 87 113 88 89 196 142 193 103 109 194 197 115 105 143 195 25 120 118 106 198 110 144 111 199 202 116 121 122 203 59 123 34 60 124 145 125 61 126 62 127 63 128 146 64 200 201 204 147 205 207 149 148 206 151 223 150 220 153 152 218 215 224 154 155 221 213 157 208 231 156 210 159 158 225 211 161 234 160 209 239 65 162 163 219 232 212 214 237 165 164 216 172 166 226 217 222 240 227 167 173 228 235 229 230 248 67 174 168 169 175 246 170 177 178 242 171 179 245 176 180 233 238 181 236 243 249 251 250 241 253 244 252 254 247 255 264 256 257 265 258 266 259 267 260 268 269 261 270 263 262 277 282 273 278 271 274 280 283 279 275 272 286 288 281 276 284 287 289 290 291 292 285 298 388 296 293 389 299 385 294 295 304 297 390 302 391 386 394 303 305 392 387 300 306 393 307 308 301 312 395 314 396 313 309 399 310 311 320 315 318 403 400 316 321 319 397 322 404 407 317 323 398 328 324 405 329 408 406 325 401 326 332 409 327 402 331 410 344 333 330 334 345 335 411 341 336 414 412 346 337 340 338 415 347 339 416 342 349 350 413 417 343 351 355 348 418 352 419 354 353 424 358 422 356 359 365 425 357 420 360 361 366 363 362 367 364 373 369 368 375 421 370 423 371 428 372 426 429 374 430 376 377 383 427 431 379 381 384 378 380 382'
BK = '075542612350344507623671114043370562142716253014657321763270437045316270540516524'


def record(core, T, topo, banks):
    rank = T.rank_of(core)
    ops = []
    cy, fix, S = PAR["cy"], PAR["fix"], SPLIT
    size = {F: 4, B: 2, H: 2, I: 4, U: 2}
    ALL = (1 << 128) - 1
    part = ["c"]

    def at(name): part[0] = name

    def v(name, a=None, b=None, s=None, p=None):
        real = "ps%d" % banks.get(name, 0) if name[0] == "#" else name
        w = SCRATCH[real][1][1]
        a = 0 if a is None else a
        b = w if b is None else b
        ps = slice(None) if p is None else slice(p[0], p[1], p[2] if len(p) > 2 else None)
        pm = ALL if p is None else sum(1 << x for x in range(128)[ps])
        return (T[real][ps, a:b:s] if s else T[real][ps, a:b], [(name, a, b, pm, a % 2 if s == 2 else None)], len(range(a, b, s or 1)),
                size[SCRATCH[real][2]], name[0] == "#")

    def blk(name, c, n=512, p=None): return v(name, n * c, n * c + n, p=p)
    def ev(n): return v(n, 0, 128, 2)
    def od(n): return v(n, 1, 128, 2)

    def z(name, half=None, u=None):
        if half is None:
            return (T[name][:], [(name, 0, 32, ALL)], 256, 2, False)
        if u is None:
            return (T[name][:, :, 16 * half:16 * half + 16], [(name, 16 * half, 16 * half + 16, ALL)], 128, 2, False)
        return (T[name][:, u, 16 * half:16 * half + 16], [(name, 16 * half, 16 * half + 16, ALL)], 16, 2, False)

    def y(name, a, b, s=1): return (T[name][:, a:b:s, :], [(name, 0, 17, ALL)], 8 * len(range(a, b, s)), 4, False)

    def ind(win, lst, c, d):
        return (T[win][:, 0:SCRATCH[win][1][1]].indirect(T[lst][:, c:d]), [(win, 0, 1 << 20, ALL), (lst, c, d, ALL)], 16 * (d - c), 4, "ind")

    def rec(q, fn, reads, writes, lat, sem=None, kind="c", busy=None, after=()):
        ops.append([q, fn, sum([r[1] for r in reads], []), sum([w[1] for w in writes], []), sem, kind, lat, lat if busy is None else busy, list(after), part[0]])
        return len(ops) - 1

    def cost(o, i, mult=1.0, half=True):
        if i[4] == "ind":
            return fix + i[2] * PAR["gather"] * cy
        if half and o[3] == 2 and i[3] == 2:
            mult = mult / 2
        return fix + max(64, i[2] * mult) * cy

    def copy(o, i): rec("v", lambda e: e.tensor_copy(o[0], i[0]), [i], [o], cost(o, i))
    def tt(o, a, b, op): rec("v", lambda e: e.tensor_tensor(o[0], a[0], b[0], op), [a, b], [o], cost(o, a, 1 if a[4] or b[4] else 2, False))
    def mset(o, c): rec("v", lambda e: e.memset(o[0], c), [], [o], cost(o, o))
    def turn(o, i): rec("v", lambda e: e.transpose(o[0], i[0]), [i], [o], cost(o, i))

    def ts(o, a, s1, op0, s2=None, op1=None):
        rd = [a] + [s for s in (s1, s2) if isinstance(s, tuple)]
        x1 = s1[0] if isinstance(s1, tuple) else s1
        if op1 is None:
            rec("v", lambda e: e.tensor_scalar(o[0], a[0], x1, None, op0), rd, [o], cost(o, a))
        else:
            rec("v", lambda e: e.tensor_scalar(o[0], a[0], x1, s2, op0, op1), rd, [o], cost(o, a))

    def act(o, i, func=None, bias=0.0, scale=1.0):
        f = AF.Identity if func is None else func
        rec("a", lambda e: e.activation(o[0], i[0], f, bias=bias, scale=scale), [i], [o], cost(o, i, 1, False))

    def lin(q, o, i, bias=0.0, scale=1.0):
        if q == "a":
            act(o, i, None, bias, scale)
        elif bias == 0.0 and scale == 1.0:
            copy(o, i)
        else:
            ts(o, i, scale, A.mult, bias, A.add)

    def relu(q, o, i):
        if q == "a":
            act(o, i, AF.Relu)
        else:
            ts(o, i, 0.0, A.max)

    def mms(calls):
        def fn(e):
            for (o, l, r, st, sp) in calls:
                ins = e.matmul(o[0], l[0], r[0], st, sp)
            return ins
        rec("p", fn, sum([[c[1], c[2]] for c in calls], []), [c[0] for c in calls],
            sum(max(min(64, l[2]), r[2]) * l[3] * l[3] / 4 * PAR["pe"] for (o, l, r, st, sp) in calls))

    def mm(o, l, r, st, sp): mms([(o, l, r, st, sp)])

    def aff(o, i, pat, cmp, base, cm): rec("g", lambda e: e.affine_select(o[0], i[0], pat, cmp, 0.0, base, cm), [i], [o], 0.17 + 2 * o[2] * cy)

    def iota(o, pat, base, cm, fl):
        if fl:
            rec("g", lambda e: e.iota(o[0], pat, base, cm, allow_small_or_imprecise_dtypes=True), [], [o], 0.13 + 2 * o[2] * cy)
        else:
            rec("g", lambda e: e.iota(o[0], pat, base, cm), [], [o], 0.13 + 2 * o[2] * cy)

    nq, nb = [0], [0]

    def dma(q, o, i, kb):
        t = kb * 1024 / PAR["bw"]
        nq[0] += 1
        rec(q, lambda e: e.dma_start(o[0], i[0]), [i], [o], PAR["dma"] + t, "q%d" % (nq[0] - 1), "d", max(0.1, t) if q == "s" else 0.1)

    def bank():
        nb[0] += 1
        return "#%d" % nb[0]

    def hbm(ap): return (ap, [])
    ROW, JROW, LROW, BL = (0, 128, 16), (1, 128, 16), (8, 128, 16), (0, 128, 8)

    pa = [T.cores[rank ^ 1], T.cores[rank ^ 2]]
    use = [e for e in topo.engines(core, pa[0]) if e in topo.engines(core, pa[1])][:8]
    emask = sum(1 << e for e in use)
    nsent = [0]

    def exchange(src, dst, r, sem, w=None):
        rid, pid, _se = topo.addr(pa[r])
        ex = 0.0 if nsent[0] else PAR["first"]
        nsent[0] += len(use)
        s_, d_ = v(src, 0, w), v(dst, 0, w)
        k = rec("g", lambda e: e.remote_dma(d_[0], s_[0], T.sem[sem], T.sem.sent, pid, rid, emask), [s_], [], PAR["rem"] + ex, "sent", "r", 0.5 + ex)
        rec("x", None, [], [d_], 0.0, sem, "x", after=[k])

    def to_list(src, dst):
        ts(z("zb", 0), src, v("mg0", 0, 1), A.mult)
        ts(z("zb", 1), src, v("mg1", 0, 1), A.mult)
        turn(z("zo"), z("zb"))
        ps = bank()
        mms([(v(ps, u, 128, 8), v("idh"), z("zo", h, u), h == 0, h == 1) for u in range(8) for h in range(2)])
        copy(v(dst), v(ps, 0, 128))

    def turned(src, n):
        ps = bank()
        for c in range(4):
            mms([(v(ps, k, 128 * n, 16), v(src, 128 * k, 128 * k + 128), v("selb", 0, 8 * n), True, True) for k in range(4 * c, 4 * c + 4)])
        return ps

    def to_block(src, n, q, prev=None):
        if prev:
            act(v("tq", 0, 128 * n), v(turned(prev, n), 0, 128 * n))
        ps = turned(src, n)
        for r in range(n):
            if prev:
                tt(blk("tp2", r, 128), blk(ps, r, 128), blk("tq", r, 128), A.max)
            else:
                lin(q, blk("tp2", r, 128), blk(ps, r, 128))

    def jlist(src, dst):
        for c in range(2):
            ps, p2, tp = bank(), bank(), "tf%d" % c
            mms([(v(ps, i, 64, 8), v(src, 1024 * c + i, 1024 * (c + 1), 8), v("selj"), True, True) for i in range(8)])
            act(y(tp, 1, 17, 2), v(ps, 0, 64))
            mms([(v(p2, 0, 64), y(tp, 1 - b, 17 - b), v("id32", b, 128, 2), b == 0, b == 1) for b in range(2)])
            copy(blk(dst, c, 64), v(p2, 0, 64))

    def jstep(out, win, lst, dst, who):
        for h in range(2):
            ps = bank()
            lin(who[h], blk(out, h, 1024), ind(win, lst, 64 * h, 64 * h + 64))
            mms([(v(ps, 0, 64), v("wd", 15 - i, 143 - i), v(out, 1024 * h + i, 1024 * (h + 1), 16), i == 0, i == 15) for i in range(16)])
            copy(blk(dst, h, 64), v(ps, 0, 64))

    def bstep(out, win, lst, keep, rows, who="vvvv"):
        for c in range(4):
            if who[c] == "v":
                tt(blk(out, c), ind(win, lst, 32 * c, 32 * c + 32), blk("bc", c), A.max)
            else:
                act(blk(out, c), ind(win, lst, 32 * c, 32 * c + 32))
            if keep[c] == "v":
                dma("s", blk("bc", c, p=rows), blk(out, c, p=rows), 16 * 16 // rows[2])

    def first_sums(x, og, who, bias, nxt, out="aa", cp="ac", kb=256):
        for c in range(4):
            d = bank()
            mms([(v(d), v("idb"), blk(x, c), True, False), (v(d), v("idb"), blk(og, c), False, True)])
            lin(who[c], blk(out, c), v(d), bias)
            if nxt[c] == "v":
                dma("s", blk(cp, c), blk(out, c), kb)

    def astep(out, win, lst, who, nxt, parts=(), gbias=0.0, bias=0.0, cp="ac"):
        for c in range(4):
            if who[c] == "v":
                tt(blk(out, c), ind(win, lst, 32 * c, 32 * c + 32), blk(cp, c), A.add)
            elif who[c] == "w":
                act(blk("gw", c), ind(win, lst, 32 * c, 32 * c + 32))
                d = bank()
                mms([(v(d), v("id32"), blk(win, c), True, False), (v(d), v("id32"), blk("gw", c), False, True)])
                act(blk(out, c), v(d))
            else:
                act(blk(parts[-1], c), ind(win, lst, 32 * c, 32 * c + 32), None, gbias)
                d = bank()
                mms([(v(d), v("idb"), blk(s_, c), n == 0, n == len(parts) - 1) for n, s_ in enumerate(parts)])
                lin("a" if who[c] == "a" else "v", blk(out, c), v(d), bias)
            if nxt[c] == "v":
                dma("s", blk("ac", c), blk(out, c), 256)

    def gather(og, x, lst, who, kind="gggg"):
        for h in range(2):
            a = 2 * h + (kind[2 * h] != "g")
            b = 2 * h + 1 + (kind[2 * h + 1] == "g")
            if a < b:
                lin(who[h], v(og, 512 * a, 512 * b), ind(x, lst, 32 * a, 32 * b))

    def gains(x, xc, lst, og, rr, kind, who):
        ps = bank()
        for c in range(4):
            if kind[c] == "f":
                tt(blk(rr, c), ind(x, lst, 32 * c, 32 * c + 32), blk(xc, c), A.max)
                tt(blk(rr, 4 + c), ind(x, lst, 128 + 32 * c, 128 + 32 * c + 32), blk(xc, c), A.max)
            else:
                d = bank()
                mms([(v(d), v("idb"), blk(x, c), True, False), (v(d), v("idn"), blk(og, c), False, True)])
                relu(who[2 * c], blk(rr, c), v(d))
                d = bank()
                mms([(v(d), v("idb"), blk(x, c), True, False),
                     (v(d, 0, 512, 2), v("idn"), v(og, 512 * c + 1, 512 * c + 512, 2), False, False),
                     (v(d, 1, 512, 2), v("idn"), v(og, 512 * c, 512 * c + 512, 2), False, True)])
                relu(who[2 * c + 1], blk(rr, 4 + c), v(d))
            mms([(v(ps, j, 64, 8), v(rr, 2048 * t + 256 * j + b, 2048 * t + 256 * j + 256, 2), v(("gmp", "gmn")[t]), t + b == 0, t + b == 2)
                 for j in range(2 * c, 2 * c + 2) for t in range(2) for b in range(2)])
        return v(ps, 0, 64)

    def halves(own, gin, side):
        tt(v("tk", 1, 129, 2), own, v(gin), A.add)
        ps = bank()
        mms([(v(ps, 0, 64), v("tk", 1 - b, 129 - b), v("ik%d" % side, 64 * b, 64 * b + 64), b == 0, b == 1) for b in range(2)])
        return v(ps, 0, 64)

    def keys(h, side):
        tt(v("t2"), h, v("nq"), A.mult)
        tt(ev("key"), v("t2"), v("ev"), A.add)
        lin(S["ko"][side], od("key"), ev("key"), float(side))
        dma("s", v("kw", p=ROW), v("key"), 64)
        dma("s", v("bc", p=ROW), v("key"), 64)

    def swap(out, src, m, d):
        tt(v("md"), v(d), v(m), A.mult)
        tt(ev(out), ev(src), v("md"), A.add)
        tt(od(out), od(src), v("md"), A.subtract)

    at("ld")
    dma("s", v("su32", 0, 128), hbm(T.su[:]), 64)
    dma("a", v("x0s"), hbm(T.x0[:]), 512)
    at("ld2")
    dma("s", v("su32", 128, 256, p=(0, 128, 2)), hbm(T.su[1:128:2, :]), 32)
    dma("s", v("su32", 128, 256, p=(1, 128, 2)), hbm(T.su[0:128:2, :]), 32)
    at("ld3")
    dma("s", v("lab32"), hbm(T.lab[:]), 64)
    dma("s", v("x0c"), hbm(T.x0[:]), 512)
    at("c1")
    mset(v("ones"), 1.0); mset(v("j0"), 0.0)
    mset(v("wd"), 0.0)
    aff(v("id32"), v("ones"), [[-1, 128]], A.is_equal, 0, 1)
    aff(v("gm1"), v("ones", 0, 8), [[-16, 8]], A.is_ge, 0, 1)
    aff(v("gm"), v("gm1"), [[16, 8]], A.is_ge, 15, -1)
    act(v("wd", 15, 143, 16), v("gm")); act(v("gmp"), v("gm")); act(v("gmn"), v("gm"), scale=-1.0)
    act(v("idb"), v("id32")); act(v("idn"), v("id32"), scale=-1.0)
    act(v("idm"), v("id32"), scale=128.0); act(v("ids"), v("id32"), scale=1.0 / 16)
    copy(v("idh"), v("id32"))
    at("c5")
    act(v("ik0"), v("id32"), scale=2048.0); act(v("ik1"), v("id32"), scale=128.0)
    mset(v("tk"), 0.0)
    act(v("in1"), v("id32"), scale=-1.0)
    tt(v("pps"), ev("id32"), od("id32"), A.add)
    tt(v("ppd"), ev("id32"), od("id32"), A.subtract)
    at("c2")
    aff(v("selb"), v("ones", 0, 16), [[-8, 2], [-16, 8]], A.is_equal, 0, 1)
    aff(v("selj"), v("ones", 0, 8), [[-16, 8]], A.is_equal, -1, 1)
    iota(v("pcol"), [[0, 4]], 0, 1, False)
    iota(v("ei"), [[2, 64]], 0, 128, False)
    ts(v("pand"), v("pcol"), 4, A.logical_shift_right, 1, A.bitwise_and)
    copy(v("mg1"), v("pand"))
    ts(v("mg0"), v("pand"), -1.0, A.mult, 1.0, A.add)
    ts(v("ei"), v("ei"), 2047, A.bitwise_and)
    copy(v("ev"), v("ei"))
    at("c3")
    for c in range(4):
        iota(blk("kw", c), [[-1, 512]], 2047 - 512 * c, 0, True)
        iota(blk("bc", c), [[0, 512]], 0, 0, True)
    dma("s", v("bc", p=LROW), v("kw", p=LROW), 64)
    at("c4")
    for n in range(2):
        mset(y("tf%d" % n, 0, 17), 0.0)

    at("ln")
    copy(v("ln", 0, 128), v("su32", 0, 128))
    copy(v("ln", 128, 256), v("su32", 128, 256))
    exchange("ln", "p1", 0, "ap1", 256 if "f" in S["par1"] else 128)
    at("ln2")
    exchange("ln", "p2", 1, "ap2", 256 if "f" in S["par2"] else 128)
    at("j0")
    ts(v("lo"), v("su32", 0, 128), 15, A.bitwise_and)
    copy(v("lob"), v("lo"))
    dma("s", v("j0", p=JROW), v("lob"), 32)
    tt(v("hib"), v("su32", 0, 128), v("lo"), A.subtract)
    dma("s", v("j0", p=ROW), v("hib"), 32)
    ps = bank()
    mms([(v(ps, 0, 128), v("idm"), v("lob"), True, False), (v(ps, 0, 128), v("ids"), v("hib"), False, True)])
    copy(v("lw"), v(ps, 0, 128))
    at("sb")
    copy(v("suh"), v("su32", 0, 128))
    ps = bank()
    mms([(v(ps, 16 * u, 16 * u + 16), v("idh"), v("suh", u, 128, 8), True, True) for u in range(8)])
    ts(z("zb", 0), v(ps, 0, 128), v("mg0", 0, 1), A.mult)
    ts(z("zb", 1), v(ps, 0, 128), v("mg1", 0, 1), A.mult)
    turn(z("zo"), z("zb"))
    tt(v("sb"), z("zo", 0), z("zo", 1), A.add)
    tt(v("ds"), od("sb"), ev("sb"), A.subtract)
    at("nq")
    tt(v("nq"), ev("lab32"), od("lab32"), A.not_equal)
    at("sb")
    tt(v("d1"), v("ds"), v("nq"), A.mult)

    beta1, beta2 = (16 * 129 - 7.5) / 8, (512 * 129 - 248) / 16
    at("og1")
    gather("og", "x0s", "ln", S["og1"])
    at("par1")
    gather("oh", "x0s", "p1", S["pg1"], S["par1"])
    gp = gains("x0s", "x0c", "p1", "oh", "mm", S["par1"], S["pr1"])
    lin(S["go"][0], v("gout1"), gp, 4096.0)
    exchange("gout1", "gin1", 0, "ag1")
    at("fs1")
    first_sums("x0s", "og", S["fs1"], beta1, S["a12"])
    at("own1")
    gs = gains("x0s", "x0c", "ln", "og", "rr", S["own1"], S["or1"])
    at("key1")
    keys(halves(gs, "gin1", 0), 0)
    at("j1")
    jstep("ja", "j0", "lw", "k1", S["j1"][0:2])
    at("j2")
    jstep("jb", "ja", "k1", "k2", S["j1"][2:4])
    at("j3")
    jstep("ja", "jb", "k2", "k3", S["j1"][4:6])
    at("b11")
    bstep("ba", "kw", "ln", "vvvv", ROW)
    at("b12")
    bstep("bb", "ba", "k1", "vvvv", ROW)
    at("b13")
    bstep("ba", "bb", "k2", S["b14"], ROW)
    at("b14")
    bstep("bb", "ba", "k3", "----", ROW, S["b14"])
    to_block("bb", 1, S["te"][0], "ba" if "a" in S["b14"] else None)
    at("a21")
    astep("ab", "aa", "k1", S["a12"], S["a13"], ["x0s", "og", "g2"], -beta1, 2 * beta1)
    at("a31")
    astep("aa", "ab", "k2", S["a13"], S["a14"], ["x0s", "og", "g2", "g3"], -2 * beta1 - 256, 4 * beta1 + 256)
    at("a41")
    astep("x1n", "aa", "k3", S["a14"], "----")
    for c in range(4):
        dma("s", blk("x1c", c), blk("x1n", c), 128)

    at("par2")
    gather("oh", "x1n", "p2", S["pg2"], S["par2"])
    gp = gains("x1n", "x1c", "p2", "oh", "mm", S["par2"], S["pr2"])
    lin(S["go"][1], v("gout2"), gp, 16 * 4096.0)
    exchange("gout2", "gin2", 1, "ag2")
    at("own2")
    gather("og", "x1n", "ln", S["og2"], S["own2"])
    gs = gains("x1n", "x1c", "ln", "og", "rr", S["own2"], S["or2"])

    at("m1")
    pt, pd = bank(), bank()
    mms([(v(pt, 0, 64), v("in1"), ev("key"), True, False), (v(pt, 0, 64), v("in1"), od("key"), False, False)])
    mm(v(pt, 0, 64), blk("tp2", 0, 128), v("pps"), False, True)
    act(v("m1"), v(pt, 0, 64), AF.Relu, 1.0, -1.0)
    at("nq2")
    mm(v(pd, 0, 64), blk("tp2", 0, 128), v("ppd"), True, True)
    ts(v("nq"), v(pd, 0, 64), 0.0, A.not_equal)
    at("m1")
    swap("sn", "sb", "m1", "d1")
    dma("s", v("kw", p=JROW), v("sn"), 64)
    to_list(v("sn"), "n0")
    at("on2")
    gather("on", "x1n", "n0", S["on2"])
    at("key2")
    keys(halves(gs, "gin2", 1), 1)

    at("fs2")
    first_sums("x1n", "on", S["fs2"], -2 * 2064.0 - 16 * 127, S["a22"], "wa", "wc", 128)
    for n, (o, w) in enumerate((("ba", "kw"), ("bb", "ba"), ("ba", "bb"), ("bb", "ba"))):
        at("b2%d" % (n + 1))
        bstep(o, w, "n%d" % n, S["b25"] if n == 3 else "vvvv", BL)
        at("jl%d" % (n + 1))
        jlist(o, "n%d" % (n + 1))
    at("b25")
    bstep("ba", "bb", "n4", "----", BL, S["b25"])
    to_block("ba", 2, S["te"][1], "bb" if "a" in S["b25"] else None)
    at("m2")
    pt, pl, pb = bank(), bank(), bank()
    mm(v(pt, 0, 64), v("in1"), ev("key"), True, False)
    mms([(v(pt, 0, 64), blk("tp2", 0, 128), ev("id32"), False, False), (v(pt, 0, 64), v("in1"), od("key"), False, False),
         (v(pt, 0, 64), blk("tp2", 0, 128), od("id32"), False, True)])
    act(v("m1"), v(pt, 0, 64), AF.Relu, 1.0, -1.0)
    mm(v(pl, 0, 128), blk("tp2", 1, 128), v("id32"), True, True)
    lin(S["ko"][2], v("lb"), v(pl, 0, 128))
    tt(v("mn"), ev("lb"), od("lb"), A.max)
    tt(v("t2"), v("mn"), v("m1"), A.mult)
    tt(ev("tb"), ev("lb"), v("t2"), A.max)
    tt(od("tb"), od("lb"), v("t2"), A.max)
    dma("s", v("kw", p=ROW), v("tb"), 64)
    at("lf")
    mm(v(pb, 0, 128), blk("tp2", 0, 128), v("id32"), True, True)
    copy(v("bi"), v(pb, 0, 128))
    ts(v("wv"), v("bi"), 2047, A.bitwise_and)
    to_list(v("wv"), "lf")
    at("ysu")
    swap("sf", "sn", "m1", "ds")
    dma("s", hbm(T.ysu[:]), v("sf"), 64)
    at("lab")
    nl = len(S["lg"])
    for h in range(nl):
        w = 2048 // nl
        lin(S["lg"][h], blk("bb", h, w), ind("kw", "lf", w // 16 * h, w // 16 * (h + 1)), 2047.0, -1.0)
        dma("s", hbm(T.ylab[:, w * h:w * (h + 1)]), blk("bb", h, w, p=ROW), 64 // nl)

    at("a22")
    astep("wb", "wa", "n1", S["a22"], "----", ["wa", "g2"], cp="wc")
    at("a32")
    astep("aa", "wb", "n2", S["a23"], S["a24"], ["wb", "g3"], 0.0, 16 * 508 + 4 * beta2)
    at("a42")
    astep("ab", "aa", "n3", S["a24"], S["a25"])
    at("a52")
    astep("yb", "ab", "n4", S["a25"], "----")
    for c in range(4):
        at("fin")
        lin(S["fin"][c], blk("yo", c), blk("yb", c), -129.0, 1.0 / 512)
        dma("s", hbm(T.yx[:, 512 * c:512 * (c + 1)]), blk("yo", c), 128)
    return ops, nsent[0], len(use)


def depend(ops):
    acc, deps = {}, []
    for n, o in enumerate(ops):
        dep = set(o[8])
        for lst, isw in ((o[2], False), (o[3], True)):
            for (name, lo, hi, p, *odd) in lst:
                for (m, l2, h2, p2, w2, odd2) in acc.get(name, []):
                    if name[0] == "#":
                        if ops[m][0] != o[0] or w2 or isw:
                            dep.add(m)
                    elif (w2 or isw) and l2 < hi and lo < h2 and p & p2 and {*odd, *odd2} != {0, 1}:
                        dep.add(m)
        dep.discard(n)
        deps.append(dep)
        for lst, isw in ((o[2], False), (o[3], True)):
            for (name, lo, hi, p, *odd) in lst:
                if name[0] == "#" and isw:
                    acc[name] = []
                elif isw and odd in ([], [None]):
                    acc[name] = [x for x in acc.get(name, []) if not (lo <= x[1] and x[2] <= hi and x[3] & ~p == 0)]
                acc.setdefault(name, []).append((n, lo, hi, p, isw, odd))
    return deps


def rank_program(g, core, T, topo):
    if T.rank_of(core) is None:
        return
    eng = {"v": g.vector, "a": g.scalar, "p": g.tensor, "g": g, "s": g.sync}
    csem = {"v": "cv", "a": "ca", "p": "cp", "g": "cg"}
    banks = {"#%d" % (n + 1): int(c) for n, c in enumerate(BK)}
    ops, nsent, nuse = record(core, T, topo, banks)
    order, deps = [int(k) for k in SEQ.split()], depend(ops)
    holder, readers = {}, {}
    for k in order:
        for a in ops[k][3]:
            if a[0] in banks and holder.get(banks[a[0]]) != a[0]:
                deps[k].update(readers.get(holder.get(banks[a[0]]), []))
                holder[banks[a[0]]] = a[0]
        for a in ops[k][2]:
            if a[0] in banks:
                readers.setdefault(a[0], []).append(k)
    pos = {k: n for n, k in enumerate(order)}
    clock = {q: {} for q in eng}
    snap, waits, need = {}, {}, set()
    for k in order:
        q = ops[k][0]
        waits[k], snap[k] = [], {}
        if q == "x":
            continue
        ck = clock[q]
        for m in sorted(deps[k], key=lambda m: -pos[m]):
            src = ops[m][4] or ops[m][0]
            if src == "sent" or (src == q == "p") or ck.get(src, -1) >= pos[m]:
                continue
            waits[k].append(m); need.add(m); ck[src] = pos[m]
            for s2, m2 in snap[m].items():
                if ck.get(s2, -1) < m2:
                    ck[s2] = m2
        snap[k] = dict(ck)
    total, count = {}, {}
    for k in order:
        o = ops[k]
        if o[5] == "c" and k in need:
            total[csem[o[0]]] = count[k] = total.get(csem[o[0]], 0) + 1
        elif o[5] == "d":
            count[k] = 16
        elif o[5] == "x":
            count[k] = nuse
    for k in order:
        q, fn, sem, kind = ops[k][0], ops[k][1], ops[k][4], ops[k][5]
        if kind == "x":
            continue
        for m in waits[k]:
            eng[q].wait_ge(T.sem[ops[m][4] or csem[ops[m][0]]], count[m])
        ins = fn(eng[q])
        if kind == "c" and k in need:
            ins.then_inc(T.sem[csem[q]], 1)
        elif kind == "d":
            ins.then_inc(T.sem[sem], 16)
    g.wait_ge(T.sem.sent, nsent)
    for k in order:
        if ops[k][5] == "d" and k not in need:
            g.wait_ge(T.sem[ops[k][4]], 16)
